import numpy as np
import ml_dtypes


def mxq(x, axis, fmt="e4m3"):
    dtype, down = {"e4m3": (ml_dtypes.float8_e4m3fn, 7), "e5m2": (ml_dtypes.float8_e5m2, 14)}[fmt]
    v = np.moveaxis(np.asarray(x, np.float32).astype(ml_dtypes.bfloat16).astype(np.float64), axis, -1)
    blocks = v.reshape(v.shape[:-1] + (-1, 32))
    amax = np.abs(blocks).max(-1, keepdims=True)
    byte = np.maximum(np.where(amax > 0, np.frexp(amax)[1] - 1 + 127, 0) - down, 1)
    scale = np.exp2(byte - 127.0)
    codes = (blocks / scale).astype(np.float32).astype(dtype).astype(np.float64)
    return np.moveaxis((codes * scale).reshape(v.shape), -1, axis)


WIDE = False


def mx_kscale(k):
    if not WIDE:
        return np.ones(k)
    levels = np.array([10, -10, 5, -5, 0])
    if k % 512:
        return np.exp2(np.random.permutation(np.resize(levels, k // 32))).repeat(32)
    a = np.empty((k // 512, 16))
    for p in range(k // 512):
        a[p, :8] = np.random.permutation(np.resize(levels, 8))
        for g in range(8):
            far = levels[np.abs(levels - a[p, g]) >= 10]
            a[p, g + 8] = far[np.random.randint(len(far))]
    return np.exp2(a.ravel()).repeat(32)


BF16 = ml_dtypes.bfloat16


def bf(x):
    return np.asarray(x, np.float32).astype(BF16)


def f64(x):
    return np.asarray(x).astype(np.float64)

def planes(Y):
    n, m = Y.shape
    b = f64(bf(Y)).reshape(n // 32, 32, m)
    amax = np.abs(b).max(1)
    byte = np.clip(np.where(amax > 0, np.frexp(amax)[1] - 1 + 127 - 7, 1), 1, 254)
    codes = (b * np.exp2(127.0 - byte)[:, None, :]).reshape(n, m).astype(np.float32).astype(ml_dtypes.float8_e4m3fn).view(np.uint8)
    words = codes.reshape(n // 512, 128, 4, m).transpose(0, 1, 3, 2)
    return np.ascontiguousarray(words), np.ascontiguousarray(byte.astype(np.uint8).reshape(n // 512, 16, m))


B, D, F, P, K = 512, 1024, 1024, 512, 3


def setup_inputs():
    u, t = mx_kscale(D), mx_kscale(F)
    return {
        "h": bf(np.random.standard_normal((B, D)) * u),
        "jac": bf(np.random.standard_normal((K, B, D)) * u),
        "lap": bf(np.random.standard_normal((B, D)) * u),
        "w1": bf(np.random.standard_normal((D, F)) / np.sqrt(D) / u[:, None]),
        "b1": bf(0.3 * np.random.standard_normal(F)),
        "g": bf((1.0 + 0.1 * np.random.standard_normal(F)) * t),
        "w2": bf(np.random.standard_normal((F, P)) / np.sqrt(F) / t[:, None]),
    }


def core(h, jac, lap, w1, b1, g, w2):
    w1q = mxq(f64(w1), 0, "e4m3")
    w2q = mxq(f64(w2), 0, "e4m3")
    gain = f64(g)

    a = np.tanh((mxq(f64(h), 1, "e4m3") @ w1q) + f64(b1)[None, :])
    s = 1.0 - a * a

    zj = mxq(f64(jac), 2, "e4m3") @ w1q
    zl = mxq(f64(lap), 1, "e4m3") @ w1q

    jn = s[None, :, :] * zj * gain[None, None, :]

    q = np.sum(zj * zj, axis=0)
    ln = (s * zl - 2.0 * a * s * q) * gain[None, :]

    jo = mxq(jn, 2, "e4m3") @ w2q
    lo = mxq(ln, 1, "e4m3") @ w2q

    return -0.5 * (lo + np.sum(jo * jo, axis=0))


def reference(h, jac, lap, w1, b1, g, w2):
    R_out = core(h, jac, lap, w1, b1, g, w2)
    words, scales = planes(R_out)
    return R_out, words, scales

@@ -1,0 +1,618 @@
+from contextlib import ExitStack
+import math
+
+import concourse.mybir as mybir
+from concourse.masks import make_identity
+
+B, D, F, PO, NJ = 512, 1024, 1024, 512, 3
+FLOPS = 2 * B * D * F * 5 + 2 * B * F * PO * 4
+
+F32 = mybir.dt.float32
+BF16 = mybir.dt.bfloat16
+U32 = mybir.dt.uint32
+I32 = mybir.dt.int32
+U8 = mybir.dt.uint8
+X4 = mybir.dt.float8_e4m3fn_x4
+ACT = mybir.ActivationFunctionType
+ALU = mybir.AluOpType
+P = 128
+NSTEP = 8
+
+
+def tile_forwardlaplaciankineticenergy_x1_kernel(tc, h, jac, lap, w1, b1, g, w2, out_0, out_1, out_2):
+    nc = tc.nc
+    with ExitStack() as ctx:
+        keep = ctx.enter_context(tc.tile_pool(name="keep", bufs=1))
+        work = ctx.enter_context(tc.tile_pool(name="work", bufs=2))
+        psum = ctx.enter_context(tc.psum_pool(name="psum", bufs=1))
+        ctx.enter_context(tc.manual_schedule())
+
+        def bank(i, name):
+            return psum.tile([P, 512], F32, name=name, tag="bank%d" % i)
+
+        ident = keep.tile([P, P], F32, name="ident")
+        b_bf = keep.tile([P, 2, 4], BF16, name="b_bf")
+        g_bf = keep.tile([P, 2, 4], BF16, name="g_bf")
+        g_neg = keep.tile([P, 2, 4], F32, name="g_neg")
+        g_pos = keep.tile([P, 2, 4], F32, name="g_pos")
+        warm = keep.tile([P, 1], F32, name="warm")
+        x_raw = keep.tile([P, 4, 5, D], BF16, name="x_raw")
+        w1_raw = keep.tile([P, 2, 2, 4, 512], BF16, name="w1_raw")
+        w2_raw = keep.tile([P, 2, 4, 512], BF16, name="w2_raw")
+        w_codes = keep.tile([P, 6, 512], U32, name="w_codes", align_bytes=64)
+        w_scales = keep.tile([P, 6, 512], U8, name="w_scales", align_bytes=64)
+        x_codes = keep.tile([P, 4, 5, 256], U32, name="x_codes", align_bytes=64)
+        x_scales = keep.tile([P, 4, 5, 256], U8, name="x_scales", align_bytes=64)
+        m_bf = keep.tile([P, 3, 4, 512], BF16, name="m_bf", align_bytes=64)
+        m_codes = keep.tile([P, NSTEP, 4, P], U32, name="m_codes", align_bytes=64)
+        m_scales = keep.tile([P, NSTEP, 4, P], U8, name="m_scales", align_bytes=64)
+        res = keep.tile([P, 4, PO], F32, name="res")
+        res_bf = keep.tile([P, PO * 4], BF16, name="res_bf", align_bytes=64)
+        res_codes = keep.tile([P, PO], U32, name="res_codes", align_bytes=64)
+        res_scales = keep.tile([P, PO], U8, name="res_scales", align_bytes=64)
+
+        def load_w1(G, kp):
+            src = w1[512 * kp : 512 * (kp + 1), 512 * G : 512 * (G + 1)]
+            nc.sync.dma_start(out=w1_raw[:, G, kp], in_=src.rearrange("(p j) c -> p j c", j=4))
+
+        def load_w2(G):
+            nc.sync.dma_start(out=w2_raw[:, G], in_=w2[512 * G : 512 * (G + 1), :].rearrange("(p j) c -> p j c", j=4))
+
+        def load_h(t):
+            nc.sync.dma_start(out=x_raw[:, t, 0], in_=h.rearrange("(p t) d -> p t d", t=4)[:, t, :])
+
+        def load_j(t, k0, k1):
+            nc.sync.dma_start(out=x_raw[:, t, 1 + k0 : 1 + k1], in_=jac.rearrange("k (p t) d -> p k t d", t=4)[:, k0:k1, t, :])
+
+        def load_l(t):
+            nc.sync.dma_start(out=x_raw[:, t, 4], in_=lap.rearrange("(p t) d -> p t d", t=4)[:, t, :])
+
+        ALUS = {"v": nc.vector, "g": nc.gpsimd}
+        w_bf = {}
+
+        def copy_on(eng, out, in_):
+            if eng == "v":
+                nc.vector.tensor_copy(out=out, in_=in_)
+            elif eng == "g":
+                nc.gpsimd.tensor_scalar(out=out, in0=in_, scalar1=1.0, scalar2=0.0, op0=ALU.mult, op1=ALU.add)
+            else:
+                nc.scalar.copy(out=out, in_=in_)
+
+        def w_inter(i, eng, half=None):
+            if i not in w_bf:
+                w_bf[i] = work.tile([P, 2048], BF16, name="w_bf%d" % i, tag="w_bf", align_bytes=64, bufs=3)
+            if i < 4:
+                dst = w_bf[i][:].rearrange("p (f m j) -> p f m j", f=4, j=4)
+                src = w1_raw[:, i // 2, i % 2].rearrange("p j (m f) -> p f m j", f=4)
+                if half is not None:
+                    dst, src = dst[:, 2 * half : 2 * half + 2], src[:, 2 * half : 2 * half + 2]
+            else:
+                dst = w_bf[i][:].rearrange("p (c i j) -> p c j i", j=4, i=4)
+                src = w2_raw[:, i - 4].rearrange("p j (c i) -> p c j i", i=4)
+                if half is not None:
+                    dst, src = dst[:, 64 * half : 64 * half + 64], src[:, 64 * half : 64 * half + 64]
+            copy_on(eng, dst, src)
+
+        def w_quant(i):
+            nc.vector.quantize_mx(out=w_codes[:, i].bitcast(X4), scales=w_scales[:, i], in_=w_bf[i][:])
+
+        x_bf = {}
+        x_ps = {}
+
+        def x_turn(t, i, bk):
+            ps = bank(bk, "xt%d_%d" % (t, i))
+            x_ps[t, i] = ps
+            words = x_raw[:, t, i].bitcast(F32)
+            for kp in range(2):
+                for u in range(2):
+                    c = (2 * kp + u) * P
+                    nc.tensor.transpose(ps[:, c : c + P], words[:, 256 * kp + u : 256 * (kp + 1) : 2], ident[:])
+
+        def x_copy(t, i, eng):
+            if t not in x_bf:
+                x_bf[t] = work.tile([P, 5 * D], BF16, name="x_bf%d" % t, tag="x_bf", align_bytes=64)
+            dst = x_bf[t][:, i * D : (i + 1) * D].bitcast(F32).rearrange("p (k b u) -> p k b u", k=2, u=2)
+            copy_on(eng, dst, x_ps[t, i][:].rearrange("p (k u b) -> p k b u", k=2, u=2))
+
+        def x_quant(t, i0, i1):
+            nc.vector.quantize_mx(
+                out=x_codes[:, t, i0:i1].rearrange("p i c -> p (i c)").bitcast(X4),
+                scales=x_scales[:, t, i0:i1].rearrange("p i c -> p (i c)"),
+                in_=x_bf[t][:, i0 * D : i1 * D],
+            )
+
+        z = {}
+
+        def z_mm(s, i, bk):
+            t, G = divmod(s, 2)
+            ps = bank(bk, "z%d_%d" % (s, i))
+            z[s, i] = ps
+            for f in range(4):
+                for kp in range(2):
+                    nc.tensor.matmul_mx(
+                        out=ps[:, f * P : (f + 1) * P],
+                        lhsT=w_codes[:, 2 * G + kp, f * P : (f + 1) * P].bitcast(X4),
+                        lhsT_scale=w_scales[:, 2 * G + kp, f * P : (f + 1) * P],
+                        rhs=x_codes[:, t, i, kp * P : (kp + 1) * P].bitcast(X4),
+                        rhs_scale=x_scales[:, t, i, kp * P : (kp + 1) * P],
+                        start=(kp == 0),
+                        stop=(kp == 1),
+                    )
+
+        def pairs(ap):
+            return ap.rearrange("p (f c i) -> p c f i", f=4, i=2)
+
+        def packed(ap):
+            return ap.rearrange("p (c i f) -> p c f i", f=4, i=2)
+
+        a, a2, sg, sq, q, m, r = {}, {}, {}, {}, {}, {}, {}
+
+        def tanh(s):
+            G = s % 2
+            a[s] = work.tile([P, 512], F32, name="a%d" % s, tag="a", bufs=3)
+            for f in range(4):
+                nc.scalar.activation(out=a[s][:, f * P : (f + 1) * P], in_=z[s, 0][:, f * P : (f + 1) * P], func=ACT.Tanh, bias=b_bf[:, G, f : f + 1])
+
+        def a_sq(s):
+            a2[s] = work.tile([P, 512], F32, name="a2_%d" % s, tag="a2")
+            nc.scalar.activation(out=a2[s][:], in_=a[s][:], func=ACT.Square)
+
+        def slope(s, eng):
+            G = s % 2
+            sg[s] = work.tile([P, 512], F32, name="sg%d" % s, tag="sg", bufs=3)
+            for f in range(4):
+                cols = slice(f * P, (f + 1) * P)
+                if eng == "s":
+                    nc.scalar.activation(out=sg[s][:, cols], in_=a2[s][:, cols], func=ACT.Identity, scale=g_neg[:, G, f : f + 1], bias=g_pos[:, G, f : f + 1])
+                else:
+                    ALUS[eng].tensor_scalar(out=sg[s][:, cols], in0=a2[s][:, cols], scalar1=g_neg[:, G, f : f + 1], scalar2=g_pos[:, G, f : f + 1], op0=ALU.mult, op1=ALU.add)
+
+        def z_sq(s, k):
+            sq[s, k] = work.tile([P, 512], F32, name="sq%d_%d" % (s, k), tag="sq%d" % k)
+            nc.scalar.activation(out=sq[s, k][:], in_=z[s, 1 + k][:], func=ACT.Square)
+
+        def jn(s, k):
+            nc.vector.tensor_tensor(out=packed(m_bf[:, s % 3, k]), in0=pairs(z[s, 1 + k][:]), in1=pairs(sg[s][:]), op=ALU.mult)
+
+        def q_add(s, k, name):
+            eng = ALUS[name]
+            if k == 1:
+                q[s] = work.tile([P, 512], F32, name="q%d" % s, tag="q", bufs=1)
+                eng.tensor_tensor(out=q[s][:], in0=sq[s, 0][:], in1=sq[s, 1][:], op=ALU.add)
+            else:
+                eng.tensor_tensor(out=q[s][:], in0=q[s][:], in1=sq[s, 2][:], op=ALU.add)
+
+        def aq(s):
+            m[s] = work.tile([P, 512], F32, name="m%d" % s, tag="m")
+            nc.vector.tensor_tensor(out=m[s][:], in0=q[s][:], in1=a[s][:], op=ALU.mult)
+
+        def lap_sum(s):
+            r[s] = work.tile([P, 512], F32, name="r%d" % s, tag="r")
+            nc.vector.scalar_tensor_tensor(
+                out=r[s][:], in0=m[s][:], scalar=-2.0, in1=z[s, 4][:], op0=ALU.mult, op1=ALU.add)
+
+        def ln(s):
+            nc.vector.tensor_tensor(out=packed(m_bf[:, s % 3, 3]), in0=pairs(r[s][:]), in1=pairs(sg[s][:]), op=ALU.mult)
+
+        def m_quant(s, k0, k1):
+            nc.vector.quantize_mx(
+                out=m_codes[:, s, k0:k1].rearrange("p k c -> p (k c)").bitcast(X4),
+                scales=m_scales[:, s, k0:k1].rearrange("p k c -> p (k c)"),
+                in_=m_bf[:, s % 3, k0:k1].rearrange("p k c -> p (k c)"),
+            )
+
+        o, e, u = {}, {}, {}
+
+        def o_mm(t, k, bk, turned):
+            ps = bank(bk, "o%d_%d" % (t, k))
+            o[t, k] = ps
+            if not turned:
+                for G in range(2):
+                    nc.tensor.matmul_mx(
+                        out=ps[:], lhsT=m_codes[:, 2 * t + G, k].bitcast(X4), lhsT_scale=m_scales[:, 2 * t + G, k],
+                        rhs=w_codes[:, 4 + G].bitcast(X4), rhs_scale=w_scales[:, 4 + G],
+                        start=(G == 0), stop=(G == 1))
+                return
+            for c in range(4):
+                cols = slice(c * P, (c + 1) * P)
+                for G in range(2):
+                    nc.tensor.matmul_mx(
+                        out=ps[:, cols], lhsT=w_codes[:, 4 + G, cols].bitcast(X4), lhsT_scale=w_scales[:, 4 + G, cols],
+                        rhs=m_codes[:, 2 * t + G, k].bitcast(X4), rhs_scale=m_scales[:, 2 * t + G, k],
+                        start=(G == 0), stop=(G == 1))
+
+        def o_sq(t, k):
+            e[t, k] = work.tile([P, PO], F32, name="e%d_%d" % (t, k), tag="e%d" % k, bufs=1)
+            nc.scalar.activation(out=e[t, k][:], in_=o[t, k][:], func=ACT.Square, scale=math.sqrt(0.5))
+
+        def turn_sum(ps, terms):
+            for c in range(4):
+                cols = slice(c * P, (c + 1) * P)
+                for n, term in enumerate(terms):
+                    nc.tensor.matmul(out=ps[:, cols], lhsT=term[:, cols], rhs=ident[:], start=(n == 0), stop=(n == len(terms) - 1), is_transpose=True)
+
+        ea, qa, qt = {}, {}, {}
+
+        def e_turn(t, bk):
+            ea[t] = bank(bk, "ea%d" % t)
+            turn_sum(ea[t], [e[t, k] for k in range(3)])
+
+        def e_copy(t):
+            u[t] = work.tile([P, PO], F32, name="u%d" % t, tag="u", bufs=1)
+            nc.scalar.copy(out=u[t][:], in_=ea[t][:])
+
+        def q_turn(s, bk):
+            qa[s] = bank(bk, "qa%d" % s)
+            turn_sum(qa[s], [sq[s, k] for k in range(3)])
+
+        def q_copy(s):
+            qt[s] = work.tile([P, 512], F32, name="qt%d" % s, tag="qt", bufs=1)
+            nc.scalar.copy(out=qt[s][:], in_=qa[s][:])
+
+        def q_back(s, bk):
+            q[s] = bank(bk, "qb%d" % s)
+            turn_sum(q[s], [qt[s]])
+
+        def e_add(t, k, name):
+            if k == 1:
+                u[t] = work.tile([P, PO], F32, name="u%d" % t, tag="u", bufs=1)
+                ALUS[name].tensor_tensor(out=u[t][:], in0=e[t, 0][:], in1=e[t, 1][:], op=ALU.add)
+            else:
+                ALUS[name].tensor_tensor(out=u[t][:], in0=u[t][:], in1=e[t, 2][:], op=ALU.add)
+
+        def finish(t, c0=0, c1=PO):
+            nc.vector.scalar_tensor_tensor(
+                out=res[:, t, c0:c1], in0=o[t, 3][:, c0:c1], scalar=-0.5, in1=u[t][:, c0:c1], op0=ALU.mult, op1=ALU.subtract)
+
+        def store(t):
+            nc.sync.dma_start(out=out_0.rearrange("(p t) m -> p t m", t=4)[:, t, :], in_=res[:, t, :])
+
+        def res_cast(c0, c1, eng):
+            copy_on(eng, res_bf[:, 4 * c0 : 4 * c1].rearrange("p (c i t) -> p c t i", t=4, i=2), res[:, :, c0:c1].rearrange("p t (c i) -> p c t i", i=2))
+
+        def res_quant(c0, c1):
+            nc.vector.quantize_mx(out=res_codes[:, c0:c1].bitcast(X4), scales=res_scales[:, c0:c1], in_=res_bf[:, 4 * c0 : 4 * c1])
+
+        make_identity(nc, ident[:])
+        nc.gpsimd.dma_start(out=b_bf[:], in_=b1.rearrange("(G p f) -> p G f", G=2, f=4))
+        nc.gpsimd.dma_start(out=g_bf[:], in_=g.rearrange("(G p f) -> p G f", G=2, f=4))
+        nc.gpsimd.tensor_scalar(out=g_neg[:], in0=g_bf[:], scalar1=-1.0, scalar2=0.0, op0=ALU.mult, op1=ALU.add)
+        nc.gpsimd.tensor_scalar(out=g_pos[:], in0=g_bf[:], scalar1=1.0, scalar2=0.0, op0=ALU.mult, op1=ALU.add)
+        load_w1(0, 1)
+        load_w1(0, 0)
+        load_h(0)
+        load_j(1, 0, 1)
+        load_j(0, 0, 1)
+        load_j(0, 2, 3)
+        load_w1(1, 1)
+        load_j(1, 1, 2)
+        load_w1(1, 0)
+        load_j(0, 1, 2)
+        load_l(0)
+        load_h(1)
+        load_l(1)
+        load_w2(0)
+        load_j(3, 2, 3)
+        load_l(2)
+        load_j(2, 0, 1)
+        load_j(1, 2, 3)
+        load_j(2, 2, 3)
+        load_l(3)
+        load_j(3, 0, 1)
+        load_h(3)
+        load_w2(1)
+        load_j(3, 1, 2)
+        load_h(2)
+        load_j(2, 1, 2)
+        nc.vector.memset(warm[:], 0.0)
+        nc.scalar.activation(out=warm[:], in_=warm[:], func=ACT.Tanh)
+        w_inter(1, "v", 0)
+        w_inter(1, "s", 1)
+        x_turn(0, 0, 0)
+        w_inter(0, "s", 1)
+        x_turn(1, 1, 1)
+        x_turn(0, 1, 2)
+        w_inter(0, "v", 0)
+        x_copy(0, 0, "s")
+        x_turn(0, 3, 3)
+        w_quant(1)
+        w_quant(0)
+        x_quant(0, 0, 1)
+        x_copy(1, 1, "s")
+        x_copy(0, 1, "v")
+        x_quant(1, 1, 2)
+        x_quant(0, 1, 2)
+        x_copy(0, 3, "s")
+        z_mm(0, 0, 4)
+        w_inter(3, "v", 1)
+        tanh(0)
+        z_mm(0, 1, 5)
+        x_quant(0, 3, 4)
+        a_sq(0)
+        w_inter(3, "v", 0)
+        x_turn(1, 2, 6)
+        z_mm(0, 3, 7)
+        w_inter(2, "v", 1)
+        w_inter(2, "s", 0)
+        z_sq(0, 2)
+        w_quant(3)
+        x_turn(0, 2, 0)
+        x_copy(1, 2, "v")
+        x_copy(0, 2, "s")
+        x_turn(0, 4, 1)
+        slope(0, "v")
+        z_sq(0, 0)
+        w_quant(2)
+        x_quant(1, 2, 3)
+        x_quant(0, 2, 3)
+        x_turn(1, 0, 2)
+        x_turn(1, 4, 3)
+        x_copy(0, 4, "s")
+        x_copy(1, 0, "s")
+        z_mm(1, 0, 4)
+        w_inter(4, "v", 0)
+        tanh(1)
+        z_mm(0, 2, 6)
+        x_quant(0, 4, 5)
+        z_mm(1, 2, 0)
+        x_turn(2, 1, 1)
+        jn(0, 2)
+        z_sq(0, 1)
+        z_sq(1, 1)
+        x_quant(1, 0, 1)
+        a_sq(1)
+        x_turn(1, 3, 2)
+        w_inter(4, "v", 1)
+        q_add(0, 1, "v")
+        x_copy(2, 1, "s")
+        z_mm(2, 0, 4)
+        w_quant(4)
+        tanh(2)
+        z_mm(1, 3, 7)
+        x_copy(1, 3, "s")
+        x_copy(1, 4, "s")
+        jn(0, 0)
+        z_mm(0, 4, 1)
+        slope(1, "v")
+        z_mm(2, 2, 4)
+        z_mm(1, 1, 2)
+        z_mm(3, 0, 3)
+        x_turn(2, 3, 5)
+        jn(0, 1)
+        q_add(0, 2, "v")
+        jn(1, 1)
+        x_turn(3, 0, 6)
+        w_inter(5, "s", 0)
+        z_sq(2, 1)
+        aq(0)
+        x_turn(3, 2, 0)
+        m_quant(0, 2, 3)
+        jn(1, 2)
+        jn(1, 0)
+        w_inter(5, "v", 1)
+        tanh(3)
+        m_quant(0, 0, 2)
+        x_copy(2, 3, "s")
+        x_turn(2, 2, 3)
+        x_turn(2, 0, 5)
+        z_sq(1, 0)
+        m_quant(1, 2, 3)
+        z_mm(2, 1, 2)
+        z_sq(1, 2)
+        x_copy(2, 0, "s")
+        x_quant(1, 4, 5)
+        lap_sum(0)
+        m_quant(1, 0, 2)
+        w_quant(5)
+        a_sq(2)
+        z_mm(3, 1, 7)
+        x_quant(1, 3, 4)
+        o_mm(0, 2, 5, True)
+        x_copy(2, 2, "s")
+        x_copy(3, 0, "s")
+        q_add(1, 1, "v")
+        x_quant(2, 3, 4)
+        z_mm(1, 4, 1)
+        o_mm(0, 1, 3, True)
+        slope(2, "v")
+        z_mm(3, 3, 6)
+        q_add(1, 2, "v")
+        x_copy(3, 2, "s")
+        a_sq(3)
+        jn(2, 1)
+        o_sq(0, 2)
+        z_mm(2, 3, 0)
+        aq(1)
+        ln(0)
+        z_mm(2, 4, 4)
+        x_quant(2, 0, 1)
+        jn(2, 2)
+        z_mm(3, 2, 5)
+        z_sq(2, 0)
+        o_sq(0, 1)
+        slope(3, "s")
+        lap_sum(1)
+        jn(2, 0)
+        z_mm(4, 0, 3)
+        jn(3, 1)
+        z_sq(2, 2)
+        z_sq(3, 2)
+        o_mm(0, 0, 1, True)
+        x_quant(2, 2, 3)
+        x_turn(3, 1, 2)
+        jn(3, 0)
+        q_add(2, 1, "v")
+        ln(1)
+        m_quant(2, 0, 2)
+        o_sq(0, 0)
+        x_turn(3, 3, 0)
+        z_sq(3, 1)
+        q_add(2, 2, "v")
+        e_turn(0, 1)
+        x_copy(3, 3, "s")
+        x_turn(2, 4, 5)
+        tanh(4)
+        m_quant(3, 0, 2)
+        z_sq(3, 0)
+        x_turn(3, 4, 0)
+        a_sq(4)
+        aq(2)
+        z_mm(5, 0, 3)
+        z_mm(4, 2, 7)
+        x_copy(3, 1, "v")
+        e_copy(0)
+        x_quant(2, 1, 2)
+        z_mm(4, 3, 2)
+        x_quant(3, 1, 2)
+        z_mm(5, 1, 1)
+        tanh(5)
+        lap_sum(2)
+        z_mm(4, 1, 3)
+        m_quant(0, 3, 4)
+        q_add(3, 1, "v")
+        jn(3, 2)
+        m_quant(1, 3, 4)
+        x_quant(3, 0, 1)
+        slope(4, "s")
+        q_add(3, 2, "v")
+        z_sq(4, 2)
+        x_copy(2, 4, "s")
+        z_sq(4, 1)
+        jn(4, 2)
+        jn(4, 1)
+        o_mm(1, 0, 4, True)
+        m_quant(3, 2, 3)
+        o_sq(1, 0)
+        z_mm(5, 2, 6)
+        x_copy(3, 4, "s")
+        x_quant(2, 4, 5)
+        o_mm(1, 1, 5, True)
+        z_sq(4, 0)
+        z_mm(6, 1, 2)
+        x_quant(3, 2, 3)
+        aq(3)
+        z_mm(6, 0, 7)
+        o_sq(1, 1)
+        m_quant(2, 2, 3)
+        jn(4, 0)
+        tanh(6)
+        z_mm(3, 4, 4)
+        o_mm(0, 3, 0, False)
+        ln(2)
+        lap_sum(3)
+        a_sq(5)
+        x_quant(3, 3, 4)
+        finish(0)
+        store(0)
+        z_mm(5, 3, 5)
+        z_sq(5, 2)
+        q_add(4, 1, "v")
+        z_mm(6, 2, 3)
+        slope(5, "s")
+        o_mm(1, 2, 7, True)
+        o_sq(1, 2)
+        z_mm(4, 4, 4)
+        jn(5, 2)
+        ln(3)
+        z_sq(5, 1)
+        q_add(4, 2, "v")
+        z_sq(5, 0)
+        m_quant(5, 2, 3)
+        a_sq(6)
+        z_mm(7, 0, 0)
+        e_turn(1, 7)
+        m_quant(3, 3, 4)
+        jn(5, 0)
+        q_turn(5, 5)
+        m_quant(2, 3, 4)
+        z_mm(5, 4, 1)
+        e_copy(1)
+        jn(5, 1)
+        m_quant(4, 2, 3)
+        aq(4)
+        z_sq(6, 1)
+        x_quant(3, 4, 5)
+        slope(6, "s")
+        q_copy(5)
+        lap_sum(4)
+        z_mm(6, 3, 7)
+        tanh(7)
+        jn(6, 0)
+        o_mm(2, 2, 6, True)
+        z_mm(7, 1, 5)
+        q_back(5, 4)
+        ln(4)
+        z_sq(6, 0)
+        z_mm(7, 2, 0)
+        a_sq(7)
+        z_sq(7, 0)
+        o_mm(1, 3, 2, False)
+        z_sq(7, 1)
+        m_quant(5, 0, 2)
+        aq(5)
+        z_sq(6, 2)
+        z_mm(7, 3, 4)
+        jn(6, 1)
+        m_quant(4, 0, 2)
+        finish(1)
+        store(1)
+        lap_sum(5)
+        z_mm(6, 4, 3)
+        o_sq(2, 2)
+        o_mm(2, 0, 2, True)
+        slope(7, "v")
+        o_mm(2, 1, 1, True)
+        z_sq(7, 2)
+        jn(6, 2)
+        o_sq(2, 0)
+        jn(7, 0)
+        o_sq(2, 1)
+        jn(7, 1)
+        ln(5)
+        jn(7, 2)
+        m_quant(7, 0, 2)
+        q_turn(6, 6)
+        m_quant(7, 2, 3)
+        q_turn(7, 7)
+        q_copy(6)
+        q_back(6, 2)
+        m_quant(6, 2, 3)
+        aq(6)
+        e_turn(2, 5)
+        m_quant(6, 0, 2)
+        m_quant(5, 3, 4)
+        lap_sum(6)
+        q_copy(7)
+        q_back(7, 1)
+        o_mm(3, 0, 0, True)
+        ln(6)
+        o_mm(3, 2, 4, True)
+        e_copy(2)
+        z_mm(7, 4, 6)
+        o_sq(3, 0)
+        o_mm(3, 1, 2, True)
+        o_sq(3, 2)
+        aq(7)
+        m_quant(6, 3, 4)
+        m_quant(4, 3, 4)
+        lap_sum(7)
+        ln(7)
+        o_sq(3, 1)
+        m_quant(7, 3, 4)
+        o_mm(2, 3, 3, False)
+        e_turn(3, 7)
+        o_mm(3, 3, 5, False)
+        finish(2)
+        store(2)
+        e_copy(3)
+        finish(3, 0, 256)
+        finish(3, 256, 512)
+        res_cast(0, 256, "s")
+        store(3)
+        res_cast(256, 512, "v")
+        res_quant(256, 512)
+        res_quant(0, 256)
+        nc.sync.dma_start(out=out_1[0].rearrange("p m t -> p (m t)").bitcast(I32), in_=res_codes[:].bitcast(I32))
+        for Q in range(4):
+            eng = nc.scalar if Q % 2 else nc.sync
+            eng.dma_start(out=out_2[0, 4 * Q : 4 * Q + 4, :].bitcast(I32), in_=res_scales[32 * Q : 32 * Q + 4, :].bitcast(I32))

@@ -278,333 +278,330 @@ def tile_forwardlaplaciankineticenergy_x1_kernel(tc, h, jac, lap, w1, b1, g, w2,
         nc.gpsimd.dma_start(out=g_bf[:], in_=g.rearrange("(G p f) -> p G f", G=2, f=4))
         nc.gpsimd.tensor_scalar(out=g_neg[:], in0=g_bf[:], scalar1=-1.0, scalar2=0.0, op0=ALU.mult, op1=ALU.add)
         nc.gpsimd.tensor_scalar(out=g_pos[:], in0=g_bf[:], scalar1=1.0, scalar2=0.0, op0=ALU.mult, op1=ALU.add)
+        load_j(0, 0, 1)
+        load_h(0)
         load_w1(0, 1)
         load_w1(0, 0)
-        load_h(0)
-        load_j(1, 0, 1)
-        load_j(0, 0, 1)
+        load_j(0, 1, 2)
         load_j(0, 2, 3)
+        load_l(1)
+        load_w1(1, 0)
         load_w1(1, 1)
         load_j(1, 1, 2)
-        load_w1(1, 0)
-        load_j(0, 1, 2)
-        load_l(0)
         load_h(1)
-        load_l(1)
+        load_j(1, 0, 1)
+        load_l(0)
         load_w2(0)
-        load_j(3, 2, 3)
-        load_l(2)
         load_j(2, 0, 1)
         load_j(1, 2, 3)
-        load_j(2, 2, 3)
-        load_l(3)
-        load_j(3, 0, 1)
+        load_l(2)
+        load_j(3, 1, 2)
         load_h(3)
         load_w2(1)
-        load_j(3, 1, 2)
-        load_h(2)
         load_j(2, 1, 2)
+        load_l(3)
+        load_j(2, 2, 3)
+        load_h(2)
+        load_j(3, 0, 1)
+        load_j(3, 2, 3)
         nc.vector.memset(warm[:], 0.0)
         nc.scalar.activation(out=warm[:], in_=warm[:], func=ACT.Tanh)
-        w_inter(1, "v", 0)
+        x_turn(0, 1, 0)
         w_inter(1, "s", 1)
-        x_turn(0, 0, 0)
-        w_inter(0, "s", 1)
-        x_turn(1, 1, 1)
-        x_turn(0, 1, 2)
-        w_inter(0, "v", 0)
-        x_copy(0, 0, "s")
-        x_turn(0, 3, 3)
-        w_quant(1)
-        w_quant(0)
-        x_quant(0, 0, 1)
-        x_copy(1, 1, "s")
+        x_turn(0, 0, 1)
         x_copy(0, 1, "v")
-        x_quant(1, 1, 2)
-        x_quant(0, 1, 2)
-        x_copy(0, 3, "s")
-        z_mm(0, 0, 4)
-        w_inter(3, "v", 1)
-        tanh(0)
-        z_mm(0, 1, 5)
-        x_quant(0, 3, 4)
-        a_sq(0)
-        w_inter(3, "v", 0)
-        x_turn(1, 2, 6)
-        z_mm(0, 3, 7)
-        w_inter(2, "v", 1)
-        w_inter(2, "s", 0)
-        z_sq(0, 2)
-        w_quant(3)
-        x_turn(0, 2, 0)
-        x_copy(1, 2, "v")
+        w_inter(1, "v", 0)
+        x_turn(0, 2, 2)
+        w_inter(0, "s", 0)
+        x_copy(0, 0, "v")
         x_copy(0, 2, "s")
-        x_turn(0, 4, 1)
-        slope(0, "v")
-        z_sq(0, 0)
-        w_quant(2)
-        x_quant(1, 2, 3)
-        x_quant(0, 2, 3)
-        x_turn(1, 0, 2)
-        x_turn(1, 4, 3)
-        x_copy(0, 4, "s")
-        x_copy(1, 0, "s")
-        z_mm(1, 0, 4)
-        w_inter(4, "v", 0)
-        tanh(1)
-        z_mm(0, 2, 6)
-        x_quant(0, 4, 5)
-        z_mm(1, 2, 0)
-        x_turn(2, 1, 1)
-        jn(0, 2)
-        z_sq(0, 1)
-        z_sq(1, 1)
-        x_quant(1, 0, 1)
-        a_sq(1)
-        x_turn(1, 3, 2)
-        w_inter(4, "v", 1)
-        q_add(0, 1, "v")
-        x_copy(2, 1, "s")
-        z_mm(2, 0, 4)
-        w_quant(4)
-        tanh(2)
-        z_mm(1, 3, 7)
-        x_copy(1, 3, "s")
+        x_turn(0, 3, 3)
+        w_inter(0, "v", 1)
+        w_quant(1)
+        x_turn(1, 4, 4)
+        x_copy(0, 3, "s")
+        x_quant(0, 1, 2)
+        w_quant(0)
         x_copy(1, 4, "s")
-        jn(0, 0)
-        z_mm(0, 4, 1)
-        slope(1, "v")
-        z_mm(2, 2, 4)
-        z_mm(1, 1, 2)
-        z_mm(3, 0, 3)
-        x_turn(2, 3, 5)
-        jn(0, 1)
-        q_add(0, 2, "v")
-        jn(1, 1)
-        x_turn(3, 0, 6)
-        w_inter(5, "s", 0)
-        z_sq(2, 1)
-        aq(0)
-        x_turn(3, 2, 0)
-        m_quant(0, 2, 3)
-        jn(1, 2)
-        jn(1, 0)
-        w_inter(5, "v", 1)
-        tanh(3)
-        m_quant(0, 0, 2)
-        x_copy(2, 3, "s")
-        x_turn(2, 2, 3)
-        x_turn(2, 0, 5)
-        z_sq(1, 0)
-        m_quant(1, 2, 3)
-        z_mm(2, 1, 2)
-        z_sq(1, 2)
-        x_copy(2, 0, "s")
+        z_mm(0, 1, 5)
+        x_quant(0, 0, 1)
+        z_sq(0, 0)
+        x_quant(0, 2, 3)
+        z_mm(0, 2, 6)
+        z_mm(0, 0, 7)
+        x_quant(0, 3, 4)
+        w_inter(2, "v", 0)
+        z_mm(0, 3, 0)
+        w_inter(3, "s", 1)
+        x_turn(1, 2, 1)
+        w_inter(2, "v", 1)
         x_quant(1, 4, 5)
+        x_turn(1, 0, 2)
+        w_inter(3, "v", 0)
+        w_quant(2)
+        x_turn(1, 1, 3)
+        z_sq(0, 1)
+        tanh(0)
+        x_copy(1, 0, "s")
+        a_sq(0)
+        w_quant(3)
+        x_turn(0, 4, 4)
+        x_copy(1, 2, "v")
+        x_copy(1, 1, "v")
+        z_mm(1, 2, 7)
+        w_inter(4, "v", 0)
+        x_quant(1, 0, 1)
+        x_copy(0, 4, "s")
+        slope(0, "v")
+        z_mm(1, 0, 2)
+        x_quant(0, 4, 5)
+        x_quant(1, 2, 3)
+        z_mm(1, 1, 1)
+        x_turn(1, 3, 3)
+        q_add(0, 1, "g")
+        z_sq(1, 1)
+        z_sq(0, 2)
+        jn(0, 1)
+        z_sq(1, 0)
+        z_mm(2, 2, 4)
+        tanh(1)
+        z_mm(2, 0, 6)
+        z_mm(1, 3, 2)
+        x_copy(1, 3, "s")
+        jn(0, 0)
+        z_mm(0, 4, 3)
+        jn(0, 2)
+        z_mm(3, 0, 5)
+        x_quant(1, 1, 2)
+        q_add(0, 2, "g")
+        a_sq(1)
+        x_turn(2, 2, 0)
+        w_inter(5, "v", 1)
+        aq(0)
+        tanh(2)
+        z_sq(1, 2)
+        m_quant(0, 0, 2)
+        tanh(3)
+        z_mm(2, 1, 6)
         lap_sum(0)
-        m_quant(1, 0, 2)
-        w_quant(5)
-        a_sq(2)
-        z_mm(3, 1, 7)
-        x_quant(1, 3, 4)
-        o_mm(0, 2, 5, True)
+        x_turn(2, 3, 5)
         x_copy(2, 2, "s")
-        x_copy(3, 0, "s")
-        q_add(1, 1, "v")
-        x_quant(2, 3, 4)
-        z_mm(1, 4, 1)
-        o_mm(0, 1, 3, True)
-        slope(2, "v")
-        z_mm(3, 3, 6)
-        q_add(1, 2, "v")
-        x_copy(3, 2, "s")
-        a_sq(3)
-        jn(2, 1)
-        o_sq(0, 2)
-        z_mm(2, 3, 0)
-        aq(1)
-        ln(0)
-        z_mm(2, 4, 4)
-        x_quant(2, 0, 1)
-        jn(2, 2)
-        z_mm(3, 2, 5)
         z_sq(2, 0)
-        o_sq(0, 1)
-        slope(3, "s")
-        lap_sum(1)
-        jn(2, 0)
-        z_mm(4, 0, 3)
-        jn(3, 1)
-        z_sq(2, 2)
-        z_sq(3, 2)
-        o_mm(0, 0, 1, True)
+        x_quant(1, 3, 4)
+        slope(1, "v")
+        ln(0)
+        x_turn(2, 0, 3)
+        m_quant(0, 2, 3)
+        q_add(1, 1, "v")
         x_quant(2, 2, 3)
-        x_turn(3, 1, 2)
-        jn(3, 0)
-        q_add(2, 1, "v")
-        ln(1)
-        m_quant(2, 0, 2)
-        o_sq(0, 0)
+        a_sq(2)
+        x_copy(2, 0, "s")
+        w_inter(4, "s", 1)
+        x_copy(2, 3, "v")
+        x_turn(2, 4, 0)
+        z_mm(2, 3, 3)
+        jn(1, 1)
+        z_sq(2, 1)
+        jn(1, 2)
+        z_mm(1, 4, 5)
+        jn(1, 0)
+        x_quant(2, 0, 1)
+        w_quant(4)
+        q_add(1, 2, "g")
+        x_copy(2, 4, "s")
+        aq(1)
+        z_mm(3, 3, 7)
+        a_sq(3)
+        slope(2, "g")
+        m_quant(1, 0, 2)
+        lap_sum(1)
+        jn(2, 1)
+        z_mm(3, 2, 2)
+        x_turn(3, 1, 1)
+        z_sq(2, 2)
+        jn(2, 0)
         x_turn(3, 3, 0)
+        jn(2, 2)
+        z_sq(3, 2)
+        x_turn(2, 1, 5)
         z_sq(3, 1)
-        q_add(2, 2, "v")
-        e_turn(0, 1)
+        x_turn(3, 0, 4)
+        w_inter(5, "s", 0)
+        z_mm(3, 1, 6)
+        z_mm(4, 2, 3)
+        ln(1)
+        x_copy(3, 1, "s")
+        w_quant(5)
         x_copy(3, 3, "s")
-        x_turn(2, 4, 5)
-        tanh(4)
-        m_quant(3, 0, 2)
-        z_sq(3, 0)
-        x_turn(3, 4, 0)
-        a_sq(4)
-        aq(2)
-        z_mm(5, 0, 3)
-        z_mm(4, 2, 7)
-        x_copy(3, 1, "v")
-        e_copy(0)
-        x_quant(2, 1, 2)
-        z_mm(4, 3, 2)
-        x_quant(3, 1, 2)
-        z_mm(5, 1, 1)
-        tanh(5)
-        lap_sum(2)
-        z_mm(4, 1, 3)
-        m_quant(0, 3, 4)
-        q_add(3, 1, "v")
+        q_add(2, 1, "g")
+        x_copy(3, 0, "s")
+        slope(3, "g")
+        m_quant(2, 0, 2)
+        q_add(2, 2, "v")
         jn(3, 2)
         m_quant(1, 3, 4)
-        x_quant(3, 0, 1)
-        slope(4, "s")
-        q_add(3, 2, "v")
-        z_sq(4, 2)
-        x_copy(2, 4, "s")
-        z_sq(4, 1)
-        jn(4, 2)
-        jn(4, 1)
-        o_mm(1, 0, 4, True)
-        m_quant(3, 2, 3)
-        o_sq(1, 0)
-        z_mm(5, 2, 6)
-        x_copy(3, 4, "s")
-        x_quant(2, 4, 5)
-        o_mm(1, 1, 5, True)
-        z_sq(4, 0)
-        z_mm(6, 1, 2)
-        x_quant(3, 2, 3)
-        aq(3)
-        z_mm(6, 0, 7)
-        o_sq(1, 1)
+        z_mm(4, 0, 1)
+        aq(2)
+        o_mm(0, 0, 0, True)
+        x_copy(2, 1, "s")
+        x_quant(2, 1, 2)
+        z_sq(3, 0)
+        x_turn(3, 4, 4)
         m_quant(2, 2, 3)
-        jn(4, 0)
-        tanh(6)
-        z_mm(3, 4, 4)
-        o_mm(0, 3, 0, False)
-        ln(2)
+        m_quant(1, 2, 3)
+        o_mm(0, 1, 7, True)
+        x_quant(2, 3, 4)
+        q_add(3, 1, "v")
+        q_add(3, 2, "g")
+        tanh(4)
+        x_copy(3, 4, "s")
+        a_sq(4)
+        z_mm(5, 0, 5)
+        x_quant(3, 0, 1)
+        z_mm(2, 4, 1)
+        o_sq(0, 0)
+        z_mm(4, 3, 4)
+        z_mm(4, 1, 0)
+        jn(3, 0)
+        jn(3, 1)
+        z_sq(4, 1)
+        lap_sum(2)
+        m_quant(3, 0, 2)
+        z_mm(3, 4, 6)
+        slope(4, "s")
+        x_quant(2, 4, 5)
+        m_quant(3, 2, 3)
+        z_sq(4, 0)
+        x_quant(3, 1, 2)
+        o_mm(0, 2, 2, True)
+        tanh(5)
+        aq(3)
+        o_sq(0, 1)
+        q_add(4, 1, "g")
+        z_mm(5, 2, 1)
+        jn(4, 1)
+        o_sq(0, 2)
+        z_sq(4, 2)
+        z_mm(6, 0, 5)
+        z_sq(5, 1)
+        z_mm(5, 1, 7)
         lap_sum(3)
+        z_mm(5, 3, 3)
         a_sq(5)
+        jn(4, 0)
+        x_turn(3, 2, 2)
+        e_turn(0, 6)
+        ln(2)
+        x_quant(3, 4, 5)
+        m_quant(0, 3, 4)
+        tanh(6)
         x_quant(3, 3, 4)
+        z_sq(5, 0)
+        o_mm(1, 2, 0, True)
+        x_copy(3, 2, "s")
+        q_add(4, 2, "v")
+        slope(5, "v")
+        m_quant(4, 0, 2)
+        z_mm(7, 0, 5)
+        e_copy(0)
+        ln(3)
+        z_mm(4, 4, 2)
+        m_quant(2, 3, 4)
+        o_sq(1, 2)
+        a_sq(6)
+        z_mm(6, 1, 6)
+        aq(4)
+        o_mm(1, 0, 0, True)
+        x_quant(3, 2, 3)
+        jn(5, 0)
+        q_add(5, 1, "g")
+        z_sq(5, 2)
+        z_mm(6, 3, 7)
+        jn(5, 1)
+        slope(6, "g")
+        jn(4, 2)
+        z_sq(6, 0)
+        lap_sum(4)
+        m_quant(3, 3, 4)
+        tanh(7)
+        q_add(5, 2, "v")
+        m_quant(4, 2, 3)
+        m_quant(5, 0, 2)
+        o_sq(1, 0)
+        o_mm(1, 1, 1, True)
+        ln(4)
+        z_mm(6, 2, 4)
+        z_sq(6, 1)
+        aq(5)
+        o_sq(1, 1)
+        jn(5, 2)
+        a_sq(7)
+        z_sq(6, 2)
+        jn(6, 0)
+        q_add(6, 1, "g")
+        o_mm(0, 3, 2, False)
+        z_mm(5, 4, 5)
+        z_mm(7, 1, 0)
+        z_mm(7, 2, 1)
+        o_mm(2, 0, 3, True)
+        jn(6, 1)
+        lap_sum(5)
         finish(0)
         store(0)
-        z_mm(5, 3, 5)
-        z_sq(5, 2)
-        q_add(4, 1, "v")
-        z_mm(6, 2, 3)
-        slope(5, "s")
-        o_mm(1, 2, 7, True)
-        o_sq(1, 2)
-        z_mm(4, 4, 4)
-        jn(5, 2)
-        ln(3)
-        z_sq(5, 1)
-        q_add(4, 2, "v")
-        z_sq(5, 0)
-        m_quant(5, 2, 3)
-        a_sq(6)
-        z_mm(7, 0, 0)
-        e_turn(1, 7)
-        m_quant(3, 3, 4)
-        jn(5, 0)
-        q_turn(5, 5)
-        m_quant(2, 3, 4)
-        z_mm(5, 4, 1)
-        e_copy(1)
-        jn(5, 1)
-        m_quant(4, 2, 3)
-        aq(4)
-        z_sq(6, 1)
-        x_quant(3, 4, 5)
-        slope(6, "s")
-        q_copy(5)
-        lap_sum(4)
-        z_mm(6, 3, 7)
-        tanh(7)
-        jn(6, 0)
-        o_mm(2, 2, 6, True)
-        z_mm(7, 1, 5)
-        q_back(5, 4)
-        ln(4)
-        z_sq(6, 0)
-        z_mm(7, 2, 0)
-        a_sq(7)
-        z_sq(7, 0)
-        o_mm(1, 3, 2, False)
         z_sq(7, 1)
-        m_quant(5, 0, 2)
-        aq(5)
-        z_sq(6, 2)
-        z_mm(7, 3, 4)
-        jn(6, 1)
-        m_quant(4, 0, 2)
+        q_add(6, 2, "g")
+        o_mm(2, 1, 6, True)
+        slope(7, "s")
+        jn(6, 2)
+        m_quant(5, 2, 3)
+        z_sq(7, 0)
+        e_turn(1, 4)
+        o_sq(2, 1)
+        z_mm(7, 3, 5)
+        e_copy(1)
+        o_sq(2, 0)
+        o_mm(2, 2, 2, True)
+        ln(5)
+        aq(6)
+        m_quant(6, 0, 2)
+        o_sq(2, 2)
+        jn(7, 1)
+        z_mm(7, 4, 7)
+        o_mm(1, 3, 6, False)
+        z_sq(7, 2)
+        jn(7, 0)
+        m_quant(6, 2, 3)
+        z_mm(6, 4, 4)
+        m_quant(4, 3, 4)
+        m_quant(5, 3, 4)
+        q_add(7, 1, "g")
+        m_quant(7, 0, 2)
+        e_turn(2, 3)
         finish(1)
         store(1)
-        lap_sum(5)
-        z_mm(6, 4, 3)
-        o_sq(2, 2)
-        o_mm(2, 0, 2, True)
-        slope(7, "v")
-        o_mm(2, 1, 1, True)
-        z_sq(7, 2)
-        jn(6, 2)
-        o_sq(2, 0)
-        jn(7, 0)
-        o_sq(2, 1)
-        jn(7, 1)
-        ln(5)
         jn(7, 2)
-        m_quant(7, 0, 2)
-        q_turn(6, 6)
-        m_quant(7, 2, 3)
-        q_turn(7, 7)
-        q_copy(6)
-        q_back(6, 2)
-        m_quant(6, 2, 3)
-        aq(6)
-        e_turn(2, 5)
-        m_quant(6, 0, 2)
-        m_quant(5, 3, 4)
+        q_add(7, 2, "g")
         lap_sum(6)
-        q_copy(7)
-        q_back(7, 1)
-        o_mm(3, 0, 0, True)
-        ln(6)
-        o_mm(3, 2, 4, True)
         e_copy(2)
-        z_mm(7, 4, 6)
-        o_sq(3, 0)
+        m_quant(7, 2, 3)
         o_mm(3, 1, 2, True)
-        o_sq(3, 2)
-        aq(7)
-        m_quant(6, 3, 4)
-        m_quant(4, 3, 4)
-        lap_sum(7)
-        ln(7)
         o_sq(3, 1)
-        m_quant(7, 3, 4)
-        o_mm(2, 3, 3, False)
-        e_turn(3, 7)
-        o_mm(3, 3, 5, False)
+        o_mm(3, 0, 1, True)
+        aq(7)
+        ln(6)
+        lap_sum(7)
+        m_quant(6, 3, 4)
+        o_mm(3, 2, 0, True)
+        o_mm(2, 3, 6, False)
+        ln(7)
         finish(2)
         store(2)
+        o_sq(3, 0)
+        o_sq(3, 2)
+        e_turn(3, 5)
         e_copy(3)
+        m_quant(7, 3, 4)
+        o_mm(3, 3, 4, False)
         finish(3, 0, 256)
         finish(3, 256, 512)
         res_cast(0, 256, "s")

@@ -44,8 +44,8 @@ def tile_forwardlaplaciankineticenergy_x1_kernel(tc, h, jac, lap, w1, b1, g, w2,
         x_codes = keep.tile([P, 4, 5, 256], U32, name="x_codes", align_bytes=64)
         x_scales = keep.tile([P, 4, 5, 256], U8, name="x_scales", align_bytes=64)
         m_bf = keep.tile([P, 3, 4, 512], BF16, name="m_bf", align_bytes=64)
-        m_codes = keep.tile([P, NSTEP, 4, P], U32, name="m_codes", align_bytes=64)
-        m_scales = keep.tile([P, NSTEP, 4, P], U8, name="m_scales", align_bytes=64)
+        m_codes = keep.tile([P, NSTEP + 1, 4, P], U32, name="m_codes", align_bytes=64)
+        m_scales = keep.tile([P, NSTEP + 1, 4, P], U8, name="m_scales", align_bytes=64)
         res = keep.tile([P, 4, PO], F32, name="res")
         res_bf = keep.tile([P, PO * 4], BF16, name="res_bf", align_bytes=64)
         res_codes = keep.tile([P, PO], U32, name="res_codes", align_bytes=64)
@@ -82,10 +82,10 @@ def tile_forwardlaplaciankineticenergy_x1_kernel(tc, h, jac, lap, w1, b1, g, w2,
             if i not in w_bf:
                 w_bf[i] = work.tile([P, 2048], BF16, name="w_bf%d" % i, tag="w_bf", align_bytes=64, bufs=3)
             if i < 4:
-                dst = w_bf[i][:].rearrange("p (f m j) -> p f m j", f=4, j=4)
-                src = w1_raw[:, i // 2, i % 2].rearrange("p j (m f) -> p f m j", f=4)
+                dst = w_bf[i][:].rearrange("p (f m j) -> p m j f", f=4, j=4)
+                src = w1_raw[:, i // 2, i % 2].rearrange("p j (m f) -> p m j f", f=4)
                 if half is not None:
-                    dst, src = dst[:, 2 * half : 2 * half + 2], src[:, 2 * half : 2 * half + 2]
+                    dst, src = dst[:, 64 * half : 64 * half + 64], src[:, 64 * half : 64 * half + 64]
             else:
                 dst = w_bf[i][:].rearrange("p (c i j) -> p c j i", j=4, i=4)
                 src = w2_raw[:, i - 4].rearrange("p j (c i) -> p c j i", i=4)
@@ -153,9 +153,12 @@ def tile_forwardlaplaciankineticenergy_x1_kernel(tc, h, jac, lap, w1, b1, g, w2,
             for f in range(4):
                 nc.scalar.activation(out=a[s][:, f * P : (f + 1) * P], in_=z[s, 0][:, f * P : (f + 1) * P], func=ACT.Tanh, bias=b_bf[:, G, f : f + 1])
 
-        def a_sq(s):
+        def a_sq(s, name):
             a2[s] = work.tile([P, 512], F32, name="a2_%d" % s, tag="a2")
-            nc.scalar.activation(out=a2[s][:], in_=a[s][:], func=ACT.Square)
+            if name == "s":
+                nc.scalar.activation(out=a2[s][:], in_=a[s][:], func=ACT.Square)
+            else:
+                nc.gpsimd.tensor_tensor(out=a2[s][:], in0=a[s][:], in1=a[s][:], op=ALU.mult)
 
         def slope(s, eng):
             G = s % 2
@@ -182,9 +185,9 @@ def tile_forwardlaplaciankineticenergy_x1_kernel(tc, h, jac, lap, w1, b1, g, w2,
             else:
                 eng.tensor_tensor(out=q[s][:], in0=q[s][:], in1=sq[s, 2][:], op=ALU.add)
 
-        def aq(s):
+        def aq(s, name):
             m[s] = work.tile([P, 512], F32, name="m%d" % s, tag="m")
-            nc.vector.tensor_tensor(out=m[s][:], in0=q[s][:], in1=a[s][:], op=ALU.mult)
+            ALUS[name].tensor_tensor(out=m[s][:], in0=q[s][:], in1=a[s][:], op=ALU.mult)
 
         def lap_sum(s):
             r[s] = work.tile([P, 512], F32, name="r%d" % s, tag="r")
@@ -192,7 +195,23 @@ def tile_forwardlaplaciankineticenergy_x1_kernel(tc, h, jac, lap, w1, b1, g, w2,
                 out=r[s][:], in0=m[s][:], scalar=-2.0, in1=z[s, 4][:], op0=ALU.mult, op1=ALU.add)
 
         def ln(s):
-            nc.vector.tensor_tensor(out=packed(m_bf[:, s % 3, 3]), in0=pairs(r[s][:]), in1=pairs(sg[s][:]), op=ALU.mult)
+            nc.vector.tensor_tensor(out=packed(m_bf[:, (s + 1) % 3, 3]), in0=pairs(r[s][:]), in1=pairs(sg[s][:]), op=ALU.mult)
+
+        def rows(ap, hf):
+            return ap.rearrange("p (f b) -> p f b", f=4)[:, :, 64 * hf : 64 * hf + 64]
+
+        def aq_half(s, hf):
+            m[s, hf] = work.tile([P, 4, 64], F32, name="mh%d" % hf, tag="mh")
+            nc.vector.tensor_tensor(out=m[s, hf][:], in0=rows(q[s][:], hf), in1=rows(a[s][:], hf), op=ALU.mult)
+
+        def lap_half(s, hf):
+            r[s, hf] = work.tile([P, 4, 64], F32, name="rh%d" % hf, tag="rh")
+            nc.vector.scalar_tensor_tensor(
+                out=r[s, hf][:], in0=m[s, hf][:], scalar=-2.0, in1=rows(z[s, 4][:], hf), op0=ALU.mult, op1=ALU.add)
+
+        def ln_half(s, hf):
+            cs = slice(32 * hf, 32 * hf + 32)
+            nc.vector.tensor_tensor(out=packed(m_bf[:, (s + 1) % 3, 3])[:, cs], in0=r[s, hf][:].rearrange("p f (c i) -> p c f i", i=2), in1=pairs(sg[s][:])[:, cs], op=ALU.mult)
 
         def m_quant(s, k0, k1):
             nc.vector.quantize_mx(
@@ -209,7 +228,7 @@ def tile_forwardlaplaciankineticenergy_x1_kernel(tc, h, jac, lap, w1, b1, g, w2,
             if not turned:
                 for G in range(2):
                     nc.tensor.matmul_mx(
-                        out=ps[:], lhsT=m_codes[:, 2 * t + G, k].bitcast(X4), lhsT_scale=m_scales[:, 2 * t + G, k],
+                        out=ps[:], lhsT=m_codes[:, 2 * t + G + k // 3, k].bitcast(X4), lhsT_scale=m_scales[:, 2 * t + G + k // 3, k],
                         rhs=w_codes[:, 4 + G].bitcast(X4), rhs_scale=w_scales[:, 4 + G],
                         start=(G == 0), stop=(G == 1))
                 return
@@ -218,7 +237,7 @@ def tile_forwardlaplaciankineticenergy_x1_kernel(tc, h, jac, lap, w1, b1, g, w2,
                 for G in range(2):
                     nc.tensor.matmul_mx(
                         out=ps[:, cols], lhsT=w_codes[:, 4 + G, cols].bitcast(X4), lhsT_scale=w_scales[:, 4 + G, cols],
-                        rhs=m_codes[:, 2 * t + G, k].bitcast(X4), rhs_scale=m_scales[:, 2 * t + G, k],
+                        rhs=m_codes[:, 2 * t + G + k // 3, k].bitcast(X4), rhs_scale=m_scales[:, 2 * t + G + k // 3, k],
                         start=(G == 0), stop=(G == 1))
 
         def o_sq(t, k):
@@ -264,8 +283,24 @@ def tile_forwardlaplaciankineticenergy_x1_kernel(tc, h, jac, lap, w1, b1, g, w2,
             nc.vector.scalar_tensor_tensor(
                 out=res[:, t, c0:c1], in0=o[t, 3][:, c0:c1], scalar=-0.5, in1=u[t][:, c0:c1], op0=ALU.mult, op1=ALU.subtract)
 
-        def store(t):
-            nc.sync.dma_start(out=out_0.rearrange("(p t) m -> p t m", t=4)[:, t, :], in_=res[:, t, :])
+        oh = {}
+
+        def o_half(hf, bk):
+            oh[hf] = bank(bk, "oh%d" % hf)
+            cols = slice(256 * hf, 256 * hf + 256)
+            for G in range(2):
+                nc.tensor.matmul_mx(
+                    out=oh[hf][:, 0:256], lhsT=m_codes[:, 7 + G, 3].bitcast(X4), lhsT_scale=m_scales[:, 7 + G, 3],
+                    rhs=w_codes[:, 4 + G, cols].bitcast(X4), rhs_scale=w_scales[:, 4 + G, cols],
+                    start=(G == 0), stop=(G == 1))
+
+        def finish_half(hf):
+            cols = slice(256 * hf, 256 * hf + 256)
+            nc.vector.scalar_tensor_tensor(
+                out=res[:, 3, cols], in0=oh[hf][:, 0:256], scalar=-0.5, in1=u[3][:, cols], op0=ALU.mult, op1=ALU.subtract)
+
+        def store(t0, t1):
+            nc.sync.dma_start(out=out_0.rearrange("(p t) m -> p t m", t=4)[:, t0:t1, :], in_=res[:, t0:t1, :])
 
         def res_cast(c0, c1, eng):
             copy_on(eng, res_bf[:, 4 * c0 : 4 * c1].rearrange("p (c i t) -> p c t i", t=4, i=2), res[:, :, c0:c1].rearrange("p t (c i) -> p c t i", i=2))
@@ -278,335 +313,318 @@ def tile_forwardlaplaciankineticenergy_x1_kernel(tc, h, jac, lap, w1, b1, g, w2,
         nc.gpsimd.dma_start(out=g_bf[:], in_=g.rearrange("(G p f) -> p G f", G=2, f=4))
         nc.gpsimd.tensor_scalar(out=g_neg[:], in0=g_bf[:], scalar1=-1.0, scalar2=0.0, op0=ALU.mult, op1=ALU.add)
         nc.gpsimd.tensor_scalar(out=g_pos[:], in0=g_bf[:], scalar1=1.0, scalar2=0.0, op0=ALU.mult, op1=ALU.add)
-        load_j(0, 0, 1)
+        load_j(0, 1, 2)
         load_h(0)
         load_w1(0, 1)
         load_w1(0, 0)
-        load_j(0, 1, 2)
+        load_j(0, 0, 1)
+        load_l(0)
+        load_h(1)
         load_j(0, 2, 3)
-        load_l(1)
         load_w1(1, 0)
         load_w1(1, 1)
         load_j(1, 1, 2)
-        load_h(1)
-        load_j(1, 0, 1)
-        load_l(0)
-        load_w2(0)
-        load_j(2, 0, 1)
         load_j(1, 2, 3)
+        load_j(1, 0, 1)
         load_l(2)
+        load_l(1)
+        load_j(2, 1, 2)
+        load_w2(0)
         load_j(3, 1, 2)
+        load_h(2)
+        load_j(3, 2, 3)
+        load_j(2, 2, 3)
         load_h(3)
         load_w2(1)
-        load_j(2, 1, 2)
-        load_l(3)
-        load_j(2, 2, 3)
-        load_h(2)
         load_j(3, 0, 1)
-        load_j(3, 2, 3)
+        load_j(2, 0, 1)
+        load_l(3)
         nc.vector.memset(warm[:], 0.0)
         nc.scalar.activation(out=warm[:], in_=warm[:], func=ACT.Tanh)
-        x_turn(0, 1, 0)
-        w_inter(1, "s", 1)
+        x_turn(0, 2, 0)
         x_turn(0, 0, 1)
-        x_copy(0, 1, "v")
+        x_turn(0, 1, 2)
+        x_turn(0, 4, 3)
+        x_copy(0, 2, "v")
+        w_inter(1, "s", 1)
         w_inter(1, "v", 0)
-        x_turn(0, 2, 2)
         w_inter(0, "s", 0)
+        x_turn(1, 0, 4)
+        x_copy(0, 1, "s")
         x_copy(0, 0, "v")
-        x_copy(0, 2, "s")
-        x_turn(0, 3, 3)
         w_inter(0, "v", 1)
         w_quant(1)
-        x_turn(1, 4, 4)
-        x_copy(0, 3, "s")
-        x_quant(0, 1, 2)
-        w_quant(0)
-        x_copy(1, 4, "s")
-        z_mm(0, 1, 5)
         x_quant(0, 0, 1)
-        z_sq(0, 0)
-        x_quant(0, 2, 3)
-        z_mm(0, 2, 6)
-        z_mm(0, 0, 7)
-        x_quant(0, 3, 4)
-        w_inter(2, "v", 0)
-        z_mm(0, 3, 0)
-        w_inter(3, "s", 1)
-        x_turn(1, 2, 1)
-        w_inter(2, "v", 1)
-        x_quant(1, 4, 5)
-        x_turn(1, 0, 2)
-        w_inter(3, "v", 0)
-        w_quant(2)
-        x_turn(1, 1, 3)
-        z_sq(0, 1)
-        tanh(0)
-        x_copy(1, 0, "s")
-        a_sq(0)
-        w_quant(3)
-        x_turn(0, 4, 4)
-        x_copy(1, 2, "v")
-        x_copy(1, 1, "v")
-        z_mm(1, 2, 7)
-        w_inter(4, "v", 0)
-        x_quant(1, 0, 1)
         x_copy(0, 4, "s")
-        slope(0, "v")
-        z_mm(1, 0, 2)
-        x_quant(0, 4, 5)
-        x_quant(1, 2, 3)
-        z_mm(1, 1, 1)
+        w_quant(0)
+        x_quant(0, 1, 3)
+        x_copy(1, 0, "s")
+        x_turn(0, 3, 5)
+        x_copy(0, 3, "s")
+        z_mm(0, 0, 6)
+        w_inter(2, "v", 0)
+        x_quant(1, 0, 1)
+        tanh(0)
+        x_quant(0, 3, 5)
+        z_mm(0, 1, 7)
+        z_mm(0, 2, 0)
+        w_inter(2, "v", 1)
+        z_sq(0, 0)
+        z_mm(2, 0, 2)
+        z_mm(0, 3, 1)
         x_turn(1, 3, 3)
-        q_add(0, 1, "g")
-        z_sq(1, 1)
+        a_sq(0, "s")
+        z_sq(0, 1)
+        w_inter(3, "s", 0)
         z_sq(0, 2)
-        jn(0, 1)
-        z_sq(1, 0)
-        z_mm(2, 2, 4)
-        tanh(1)
-        z_mm(2, 0, 6)
-        z_mm(1, 3, 2)
-        x_copy(1, 3, "s")
-        jn(0, 0)
-        z_mm(0, 4, 3)
-        jn(0, 2)
-        z_mm(3, 0, 5)
-        x_quant(1, 1, 2)
-        q_add(0, 2, "g")
-        a_sq(1)
-        x_turn(2, 2, 0)
-        w_inter(5, "v", 1)
-        aq(0)
+        x_turn(1, 1, 4)
         tanh(2)
-        z_sq(1, 2)
-        m_quant(0, 0, 2)
-        tanh(3)
-        z_mm(2, 1, 6)
-        lap_sum(0)
-        x_turn(2, 3, 5)
-        x_copy(2, 2, "s")
-        z_sq(2, 0)
-        x_quant(1, 3, 4)
-        slope(1, "v")
-        ln(0)
-        x_turn(2, 0, 3)
+        w_inter(3, "v", 1)
+        x_copy(1, 3, "s")
+        w_quant(2)
+        q_add(0, 1, "v")
+        x_turn(1, 4, 5)
+        x_turn(1, 2, 6)
+        slope(0, "v")
+        w_quant(3)
+        z_mm(1, 1, 2)
+        z_mm(1, 0, 3)
+        x_copy(1, 1, "s")
+        q_add(0, 2, "v")
+        x_copy(1, 2, "s")
+        x_copy(1, 4, "s")
+        w_inter(4, "v", 0)
+        jn(0, 2)
+        jn(0, 0)
+        aq(0, "g")
+        x_turn(2, 0, 4)
+        tanh(1)
+        jn(0, 1)
+        z_mm(0, 4, 6)
+        z_mm(3, 0, 5)
         m_quant(0, 2, 3)
-        q_add(1, 1, "v")
-        x_quant(2, 2, 3)
-        a_sq(2)
-        x_copy(2, 0, "s")
-        w_inter(4, "s", 1)
-        x_copy(2, 3, "v")
-        x_turn(2, 4, 0)
-        z_mm(2, 3, 3)
-        jn(1, 1)
-        z_sq(2, 1)
-        jn(1, 2)
-        z_mm(1, 4, 5)
-        jn(1, 0)
-        x_quant(2, 0, 1)
+        w_inter(4, "v", 1)
+        x_quant(1, 1, 5)
+        lap_sum(0)
+        a_sq(2, "s")
+        z_mm(1, 3, 1)
+        x_copy(2, 0, "v")
+        z_mm(1, 2, 7)
+        x_turn(2, 4, 3)
+        a_sq(1, "s")
         w_quant(4)
-        q_add(1, 2, "g")
+        x_turn(2, 2, 0)
+        tanh(3)
+        z_mm(2, 2, 6)
+        z_mm(2, 1, 4)
+        z_sq(1, 0)
+        z_sq(1, 1)
+        q_add(1, 1, "v")
         x_copy(2, 4, "s")
-        aq(1)
-        z_mm(3, 3, 7)
-        a_sq(3)
-        slope(2, "g")
-        m_quant(1, 0, 2)
-        lap_sum(1)
-        jn(2, 1)
-        z_mm(3, 2, 2)
-        x_turn(3, 1, 1)
-        z_sq(2, 2)
-        jn(2, 0)
-        x_turn(3, 3, 0)
-        jn(2, 2)
-        z_sq(3, 2)
-        x_turn(2, 1, 5)
-        z_sq(3, 1)
-        x_turn(3, 0, 4)
-        w_inter(5, "s", 0)
-        z_mm(3, 1, 6)
-        z_mm(4, 2, 3)
-        ln(1)
-        x_copy(3, 1, "s")
-        w_quant(5)
-        x_copy(3, 3, "s")
-        q_add(2, 1, "g")
-        x_copy(3, 0, "s")
-        slope(3, "g")
-        m_quant(2, 0, 2)
-        q_add(2, 2, "v")
-        jn(3, 2)
-        m_quant(1, 3, 4)
-        z_mm(4, 0, 1)
-        aq(2)
-        o_mm(0, 0, 0, True)
-        x_copy(2, 1, "s")
-        x_quant(2, 1, 2)
-        z_sq(3, 0)
-        x_turn(3, 4, 4)
-        m_quant(2, 2, 3)
-        m_quant(1, 2, 3)
-        o_mm(0, 1, 7, True)
-        x_quant(2, 3, 4)
-        q_add(3, 1, "v")
-        q_add(3, 2, "g")
-        tanh(4)
+        z_sq(1, 2)
+        z_mm(2, 3, 5)
+        slope(1, "g")
+        z_mm(1, 4, 3)
+        m_quant(0, 0, 2)
+        jn(1, 2)
+        slope(2, "s")
+        x_copy(2, 2, "s")
+        x_turn(3, 4, 1)
+        x_turn(2, 1, 0)
+        jn(1, 0)
+        jn(1, 1)
+        a_sq(3, "s")
+        x_quant(2, 0, 1)
+        q_add(1, 2, "g")
+        z_sq(2, 0)
+        z_sq(2, 1)
+        w_inter(5, "v", 0)
         x_copy(3, 4, "s")
-        a_sq(4)
-        z_mm(5, 0, 5)
-        x_quant(3, 0, 1)
-        z_mm(2, 4, 1)
-        o_sq(0, 0)
-        z_mm(4, 3, 4)
-        z_mm(4, 1, 0)
-        jn(3, 0)
-        jn(3, 1)
-        z_sq(4, 1)
-        lap_sum(2)
-        m_quant(3, 0, 2)
-        z_mm(3, 4, 6)
-        slope(4, "s")
-        x_quant(2, 4, 5)
-        m_quant(3, 2, 3)
-        z_sq(4, 0)
-        x_quant(3, 1, 2)
+        aq(1, "v")
+        ln(0)
+        jn(2, 1)
+        q_add(2, 1, "g")
+        z_sq(2, 2)
+        x_turn(3, 3, 2)
+        jn(2, 0)
+        lap_sum(1)
+        x_turn(2, 3, 7)
+        m_quant(1, 0, 4)
+        z_mm(3, 2, 1)
+        z_mm(4, 0, 6)
+        w_inter(5, "s", 1)
+        x_copy(2, 3, "s")
+        ln(1)
+        x_turn(3, 1, 4)
+        w_quant(5)
+        tanh(4)
+        x_turn(3, 0, 3)
+        x_turn(3, 2, 7)
+        q_add(2, 2, "v")
+        x_copy(2, 1, "s")
+        z_mm(3, 1, 6)
+        slope(3, "s")
+        z_mm(3, 3, 0)
+        x_copy(3, 3, "s")
+        aq(2, "g")
         o_mm(0, 2, 2, True)
-        tanh(5)
-        aq(3)
-        o_sq(0, 1)
-        q_add(4, 1, "g")
-        z_mm(5, 2, 1)
-        jn(4, 1)
-        o_sq(0, 2)
-        z_sq(4, 2)
-        z_mm(6, 0, 5)
-        z_sq(5, 1)
-        z_mm(5, 1, 7)
-        lap_sum(3)
-        z_mm(5, 3, 3)
-        a_sq(5)
-        jn(4, 0)
-        x_turn(3, 2, 2)
-        e_turn(0, 6)
-        ln(2)
-        x_quant(3, 4, 5)
-        m_quant(0, 3, 4)
-        tanh(6)
-        x_quant(3, 3, 4)
-        z_sq(5, 0)
-        o_mm(1, 2, 0, True)
+        x_quant(2, 1, 5)
+        x_copy(3, 0, "s")
+        z_mm(2, 4, 3)
+        x_copy(3, 1, "s")
+        z_sq(3, 1)
+        o_mm(0, 1, 4, True)
+        jn(3, 2)
+        jn(2, 2)
+        jn(3, 1)
+        lap_sum(2)
+        z_sq(3, 0)
+        z_mm(5, 3, 5)
         x_copy(3, 2, "s")
-        q_add(4, 2, "v")
-        slope(5, "v")
-        m_quant(4, 0, 2)
-        z_mm(7, 0, 5)
+        o_sq(0, 2)
+        z_sq(3, 2)
+        z_mm(4, 2, 1)
+        jn(3, 0)
+        o_mm(0, 0, 3, True)
+        q_add(3, 1, "g")
+        a_sq(4, "s")
+        o_sq(0, 1)
+        z_mm(4, 1, 7)
+        slope(4, "s")
+        ln(2)
+        z_mm(5, 2, 2)
+        o_sq(0, 0)
+        q_add(3, 2, "v")
+        z_sq(4, 1)
+        z_mm(5, 0, 0)
+        z_mm(3, 4, 6)
+        x_quant(3, 1, 5)
+        tanh(5)
+        aq(3, "v")
+        m_quant(3, 0, 4)
+        z_mm(4, 3, 4)
+        e_turn(0, 3)
+        m_quant(2, 0, 4)
+        x_quant(3, 0, 1)
+        jn(4, 1)
+        z_sq(4, 0)
+        jn(4, 0)
+        a_sq(5, "s")
+        lap_sum(3)
+        z_sq(4, 2)
+        z_mm(5, 1, 0)
+        q_add(4, 1, "g")
+        o_mm(1, 0, 1, True)
+        slope(5, "s")
+        z_mm(6, 2, 7)
         e_copy(0)
-        ln(3)
-        z_mm(4, 4, 2)
-        m_quant(2, 3, 4)
-        o_sq(1, 2)
-        a_sq(6)
-        z_mm(6, 1, 6)
-        aq(4)
-        o_mm(1, 0, 0, True)
-        x_quant(3, 2, 3)
-        jn(5, 0)
-        q_add(5, 1, "g")
-        z_sq(5, 2)
-        z_mm(6, 3, 7)
-        jn(5, 1)
-        slope(6, "g")
-        jn(4, 2)
-        z_sq(6, 0)
-        lap_sum(4)
-        m_quant(3, 3, 4)
-        tanh(7)
-        q_add(5, 2, "v")
-        m_quant(4, 2, 3)
-        m_quant(5, 0, 2)
+        z_mm(4, 4, 6)
+        q_add(4, 2, "v")
         o_sq(1, 0)
+        ln(3)
+        z_mm(6, 0, 3)
+        aq(4, "g")
+        z_sq(5, 0)
+        jn(4, 2)
+        jn(5, 0)
+        z_sq(5, 1)
         o_mm(1, 1, 1, True)
-        ln(4)
-        z_mm(6, 2, 4)
+        jn(5, 1)
         z_sq(6, 1)
-        aq(5)
+        z_sq(5, 2)
+        lap_sum(4)
+        o_mm(1, 2, 4, True)
+        tanh(6)
+        z_mm(7, 0, 0)
         o_sq(1, 1)
+        z_mm(7, 3, 2)
+        a_sq(6, "s")
+        z_mm(6, 3, 6)
+        q_add(5, 1, "g")
+        z_mm(5, 4, 3)
+        o_mm(0, 3, 1, False)
         jn(5, 2)
-        a_sq(7)
-        z_sq(6, 2)
-        jn(6, 0)
-        q_add(6, 1, "g")
-        o_mm(0, 3, 2, False)
-        z_mm(5, 4, 5)
-        z_mm(7, 1, 0)
-        z_mm(7, 2, 1)
-        o_mm(2, 0, 3, True)
-        jn(6, 1)
-        lap_sum(5)
+        ln(4)
+        tanh(7)
+        m_quant(4, 0, 4)
+        q_add(5, 2, "v")
+        aq(5, "g")
+        m_quant(5, 0, 4)
         finish(0)
-        store(0)
-        z_sq(7, 1)
-        q_add(6, 2, "g")
-        o_mm(2, 1, 6, True)
-        slope(7, "s")
+        store(0, 1)
+        z_mm(6, 1, 5)
+        slope(6, "s")
+        o_sq(1, 2)
         jn(6, 2)
-        m_quant(5, 2, 3)
-        z_sq(7, 0)
+        a_sq(7, "s")
+        z_mm(7, 2, 0)
+        z_mm(7, 1, 1)
+        jn(6, 1)
+        z_sq(6, 0)
+        lap_sum(5)
         e_turn(1, 4)
-        o_sq(2, 1)
-        z_mm(7, 3, 5)
-        e_copy(1)
-        o_sq(2, 0)
-        o_mm(2, 2, 2, True)
-        ln(5)
-        aq(6)
-        m_quant(6, 0, 2)
-        o_sq(2, 2)
-        jn(7, 1)
-        z_mm(7, 4, 7)
-        o_mm(1, 3, 6, False)
-        z_sq(7, 2)
-        jn(7, 0)
-        m_quant(6, 2, 3)
-        z_mm(6, 4, 4)
-        m_quant(4, 3, 4)
-        m_quant(5, 3, 4)
-        q_add(7, 1, "g")
-        m_quant(7, 0, 2)
-        e_turn(2, 3)
-        finish(1)
-        store(1)
+        jn(6, 0)
+        slope(7, "s")
+        o_mm(2, 1, 7, True)
+        z_sq(6, 2)
+        q_add(6, 1, "g")
         jn(7, 2)
-        q_add(7, 2, "g")
-        lap_sum(6)
-        e_copy(2)
+        z_sq(7, 0)
+        jn(7, 1)
+        q_add(6, 2, "g")
+        jn(7, 0)
+        o_mm(2, 0, 3, True)
+        z_mm(6, 4, 5)
+        o_mm(2, 2, 6, True)
+        ln(5)
+        o_sq(2, 1)
+        o_sq(2, 0)
+        z_sq(7, 1)
+        o_mm(1, 3, 1, False)
         m_quant(7, 2, 3)
-        o_mm(3, 1, 2, True)
-        o_sq(3, 1)
-        o_mm(3, 0, 1, True)
-        aq(7)
-        ln(6)
-        lap_sum(7)
-        m_quant(6, 3, 4)
+        aq(6, "v")
+        o_sq(2, 2)
+        e_copy(1)
+        z_sq(7, 2)
+        z_mm(7, 4, 7)
+        m_quant(6, 0, 4)
+        lap_sum(6)
+        q_add(7, 1, "g")
+        finish(1)
+        store(1, 2)
+        e_turn(2, 3)
+        m_quant(7, 1, 2)
+        m_quant(7, 0, 1)
+        q_add(7, 2, "v")
         o_mm(3, 2, 0, True)
-        o_mm(2, 3, 6, False)
-        ln(7)
-        finish(2)
-        store(2)
-        o_sq(3, 0)
+        o_mm(3, 1, 6, True)
+        o_mm(3, 0, 4, True)
+        ln(6)
+        aq_half(7, 1)
+        aq_half(7, 0)
+        lap_half(7, 1)
+        o_mm(2, 3, 2, False)
+        e_copy(2)
+        lap_half(7, 0)
         o_sq(3, 2)
+        ln_half(7, 1)
+        o_sq(3, 1)
+        ln_half(7, 0)
+        finish(2)
+        o_sq(3, 0)
         e_turn(3, 5)
-        e_copy(3)
+        m_quant(8, 3, 4)
         m_quant(7, 3, 4)
-        o_mm(3, 3, 4, False)
-        finish(3, 0, 256)
-        finish(3, 256, 512)
-        res_cast(0, 256, "s")
-        store(3)
-        res_cast(256, 512, "v")
+        e_copy(3)
+        o_half(1, 1)
+        finish_half(1)
+        o_half(0, 3)
+        finish_half(0)
+        store(2, 4)
+        res_cast(256, 384, "v")
+        res_cast(384, 512, "s")
+        res_cast(128, 256, "v")
+        res_cast(0, 128, "v")
         res_quant(256, 512)
         res_quant(0, 256)
         nc.sync.dma_start(out=out_1[0].rearrange("p m t -> p (m t)").bitcast(I32), in_=res_codes[:].bitcast(I32))

@@ -30,6 +30,7 @@ def tile_forwardlaplaciankineticenergy_x1_kernel(tc, h, jac, lap, w1, b1, g, w2,
         def bank(i, name):
             return psum.tile([P, 512], F32, name=name, tag="bank%d" % i)
 
+        zeros = keep.tile([P, 512], BF16, name="zeros")
         ident = keep.tile([P, P], F32, name="ident")
         b_bf = keep.tile([P, 2, 4], BF16, name="b_bf")
         g_bf = keep.tile([P, 2, 4], BF16, name="g_bf")
@@ -68,6 +69,12 @@ def tile_forwardlaplaciankineticenergy_x1_kernel(tc, h, jac, lap, w1, b1, g, w2,
             nc.sync.dma_start(out=x_raw[:, t, 4], in_=lap.rearrange("(p t) d -> p t d", t=4)[:, t, :])
 
         ALUS = {"v": nc.vector, "g": nc.gpsimd}
+        idle_bank = bank(7, "idle_bank")
+
+        def keep_warm(n):
+            for i in range(n):
+                nc.tensor.matmul(out=idle_bank[:], lhsT=zeros[:, 0:P], rhs=zeros[:], start=True, stop=True)
+
         w_bf = {}
 
         def copy_on(eng, out, in_):
@@ -339,12 +346,17 @@ def tile_forwardlaplaciankineticenergy_x1_kernel(tc, h, jac, lap, w1, b1, g, w2,
         load_j(3, 0, 1)
         load_j(2, 0, 1)
         load_l(3)
+        nc.vector.memset(zeros[:], 0.0)
         nc.vector.memset(warm[:], 0.0)
+        keep_warm(4)
         nc.scalar.activation(out=warm[:], in_=warm[:], func=ACT.Tanh)
         x_turn(0, 2, 0)
+        keep_warm(1)
         x_turn(0, 0, 1)
+        keep_warm(7)
         x_turn(0, 1, 2)
         x_turn(0, 4, 3)
+        keep_warm(1)
         x_copy(0, 2, "v")
         w_inter(1, "s", 1)
         w_inter(1, "v", 0)

from contextlib import ExitStack
import math

import concourse.mybir as mybir
from concourse.masks import make_identity

B, D, F, PO, NJ = 512, 1024, 1024, 512, 3
FLOPS = 2 * B * D * F * 5 + 2 * B * F * PO * 4

F32 = mybir.dt.float32
BF16 = mybir.dt.bfloat16
U32 = mybir.dt.uint32
I32 = mybir.dt.int32
U8 = mybir.dt.uint8
X4 = mybir.dt.float8_e4m3fn_x4
ACT = mybir.ActivationFunctionType
ALU = mybir.AluOpType
P = 128
NSTEP = 8


def tile_forwardlaplaciankineticenergy_x1_kernel(tc, h, jac, lap, w1, b1, g, w2, out_0, out_1, out_2):
    nc = tc.nc
    with ExitStack() as ctx:
        keep = ctx.enter_context(tc.tile_pool(name="keep", bufs=1))
        work = ctx.enter_context(tc.tile_pool(name="work", bufs=2))
        psum = ctx.enter_context(tc.psum_pool(name="psum", bufs=1))
        ctx.enter_context(tc.manual_schedule())

        def bank(i, name):
            return psum.tile([P, 512], F32, name=name, tag="bank%d" % i)

        zeros = keep.tile([P, 512], BF16, name="zeros")
        ident = keep.tile([P, P], F32, name="ident")
        b_bf = keep.tile([P, 2, 4], BF16, name="b_bf")
        g_bf = keep.tile([P, 2, 4], BF16, name="g_bf")
        g_neg = keep.tile([P, 2, 4], F32, name="g_neg")
        g_pos = keep.tile([P, 2, 4], F32, name="g_pos")
        warm = keep.tile([P, 1], F32, name="warm")
        x_raw = keep.tile([P, 4, 5, D], BF16, name="x_raw")
        w1_raw = keep.tile([P, 2, 2, 4, 512], BF16, name="w1_raw")
        w2_raw = keep.tile([P, 2, 4, 512], BF16, name="w2_raw")
        w_codes = keep.tile([P, 6, 512], U32, name="w_codes", align_bytes=64)
        w_scales = keep.tile([P, 6, 512], U8, name="w_scales", align_bytes=64)
        x_codes = keep.tile([P, 4, 5, 256], U32, name="x_codes", align_bytes=64)
        x_scales = keep.tile([P, 4, 5, 256], U8, name="x_scales", align_bytes=64)
        m_bf = keep.tile([P, 3, 4, 512], BF16, name="m_bf", align_bytes=64)
        m_codes = keep.tile([P, NSTEP + 1, 4, P], U32, name="m_codes", align_bytes=64)
        m_scales = keep.tile([P, NSTEP + 1, 4, P], U8, name="m_scales", align_bytes=64)
        res = keep.tile([P, 4, PO], F32, name="res")
        res_bf = keep.tile([P, PO * 4], BF16, name="res_bf", align_bytes=64)
        res_codes = keep.tile([P, PO], U32, name="res_codes", align_bytes=64)
        res_scales = keep.tile([P, PO], U8, name="res_scales", align_bytes=64)

        def load_w1(G, kp):
            src = w1[512 * kp : 512 * (kp + 1), 512 * G : 512 * (G + 1)]
            nc.sync.dma_start(out=w1_raw[:, G, kp], in_=src.rearrange("(p j) c -> p j c", j=4))

        def load_w2(G):
            nc.sync.dma_start(out=w2_raw[:, G], in_=w2[512 * G : 512 * (G + 1), :].rearrange("(p j) c -> p j c", j=4))

        def load_h(t):
            nc.sync.dma_start(out=x_raw[:, t, 0], in_=h.rearrange("(p t) d -> p t d", t=4)[:, t, :])

        def load_j(t, k0, k1):
            nc.sync.dma_start(out=x_raw[:, t, 1 + k0 : 1 + k1], in_=jac.rearrange("k (p t) d -> p k t d", t=4)[:, k0:k1, t, :])

        def load_l(t):
            nc.sync.dma_start(out=x_raw[:, t, 4], in_=lap.rearrange("(p t) d -> p t d", t=4)[:, t, :])

        ALUS = {"v": nc.vector, "g": nc.gpsimd}
        idle_bank = bank(7, "idle_bank")

        def keep_warm(n):
            for i in range(n):
                nc.tensor.matmul(out=idle_bank[:], lhsT=zeros[:, 0:P], rhs=zeros[:], start=True, stop=True)

        w_bf = {}

        def copy_on(eng, out, in_):
            if eng == "v":
                nc.vector.tensor_copy(out=out, in_=in_)
            elif eng == "g":
                nc.gpsimd.tensor_scalar(out=out, in0=in_, scalar1=1.0, scalar2=0.0, op0=ALU.mult, op1=ALU.add)
            else:
                nc.scalar.copy(out=out, in_=in_)

        def w_inter(i, eng, half=None):
            if i not in w_bf:
                w_bf[i] = work.tile([P, 2048], BF16, name="w_bf%d" % i, tag="w_bf", align_bytes=64, bufs=3)
            if i < 4:
                dst = w_bf[i][:].rearrange("p (f m j) -> p m j f", f=4, j=4)
                src = w1_raw[:, i // 2, i % 2].rearrange("p j (m f) -> p m j f", f=4)
                if half is not None:
                    dst, src = dst[:, 64 * half : 64 * half + 64], src[:, 64 * half : 64 * half + 64]
            else:
                dst = w_bf[i][:].rearrange("p (c i j) -> p c j i", j=4, i=4)
                src = w2_raw[:, i - 4].rearrange("p j (c i) -> p c j i", i=4)
                if half is not None:
                    dst, src = dst[:, 64 * half : 64 * half + 64], src[:, 64 * half : 64 * half + 64]
            copy_on(eng, dst, src)

        def w_quant(i):
            nc.vector.quantize_mx(out=w_codes[:, i].bitcast(X4), scales=w_scales[:, i], in_=w_bf[i][:])

        x_bf = {}
        x_ps = {}

        def x_turn(t, i, bk):
            ps = bank(bk, "xt%d_%d" % (t, i))
            x_ps[t, i] = ps
            words = x_raw[:, t, i].bitcast(F32)
            for kp in range(2):
                for u in range(2):
                    c = (2 * kp + u) * P
                    nc.tensor.transpose(ps[:, c : c + P], words[:, 256 * kp + u : 256 * (kp + 1) : 2], ident[:])

        def x_copy(t, i, eng):
            if t not in x_bf:
                x_bf[t] = work.tile([P, 5 * D], BF16, name="x_bf%d" % t, tag="x_bf", align_bytes=64)
            dst = x_bf[t][:, i * D : (i + 1) * D].bitcast(F32).rearrange("p (k b u) -> p k b u", k=2, u=2)
            copy_on(eng, dst, x_ps[t, i][:].rearrange("p (k u b) -> p k b u", k=2, u=2))

        def x_quant(t, i0, i1):
            nc.vector.quantize_mx(
                out=x_codes[:, t, i0:i1].rearrange("p i c -> p (i c)").bitcast(X4),
                scales=x_scales[:, t, i0:i1].rearrange("p i c -> p (i c)"),
                in_=x_bf[t][:, i0 * D : i1 * D],
            )

        z = {}

        def z_mm(s, i, bk):
            t, G = divmod(s, 2)
            ps = bank(bk, "z%d_%d" % (s, i))
            z[s, i] = ps
            for f in range(4):
                for kp in range(2):
                    nc.tensor.matmul_mx(
                        out=ps[:, f * P : (f + 1) * P],
                        lhsT=w_codes[:, 2 * G + kp, f * P : (f + 1) * P].bitcast(X4),
                        lhsT_scale=w_scales[:, 2 * G + kp, f * P : (f + 1) * P],
                        rhs=x_codes[:, t, i, kp * P : (kp + 1) * P].bitcast(X4),
                        rhs_scale=x_scales[:, t, i, kp * P : (kp + 1) * P],
                        start=(kp == 0),
                        stop=(kp == 1),
                    )

        def pairs(ap):
            return ap.rearrange("p (f c i) -> p c f i", f=4, i=2)

        def packed(ap):
            return ap.rearrange("p (c i f) -> p c f i", f=4, i=2)

        a, a2, sg, sq, q, m, r = {}, {}, {}, {}, {}, {}, {}

        def tanh(s):
            G = s % 2
            a[s] = work.tile([P, 512], F32, name="a%d" % s, tag="a", bufs=3)
            for f in range(4):
                nc.scalar.activation(out=a[s][:, f * P : (f + 1) * P], in_=z[s, 0][:, f * P : (f + 1) * P], func=ACT.Tanh, bias=b_bf[:, G, f : f + 1])

        def a_sq(s, name):
            a2[s] = work.tile([P, 512], F32, name="a2_%d" % s, tag="a2")
            if name == "s":
                nc.scalar.activation(out=a2[s][:], in_=a[s][:], func=ACT.Square)
            else:
                nc.gpsimd.tensor_tensor(out=a2[s][:], in0=a[s][:], in1=a[s][:], op=ALU.mult)

        def slope(s, eng):
            G = s % 2
            sg[s] = work.tile([P, 512], F32, name="sg%d" % s, tag="sg", bufs=3)
            for f in range(4):
                cols = slice(f * P, (f + 1) * P)
                if eng == "s":
                    nc.scalar.activation(out=sg[s][:, cols], in_=a2[s][:, cols], func=ACT.Identity, scale=g_neg[:, G, f : f + 1], bias=g_pos[:, G, f : f + 1])
                else:
                    ALUS[eng].tensor_scalar(out=sg[s][:, cols], in0=a2[s][:, cols], scalar1=g_neg[:, G, f : f + 1], scalar2=g_pos[:, G, f : f + 1], op0=ALU.mult, op1=ALU.add)

        def z_sq(s, k):
            sq[s, k] = work.tile([P, 512], F32, name="sq%d_%d" % (s, k), tag="sq%d" % k)
            nc.scalar.activation(out=sq[s, k][:], in_=z[s, 1 + k][:], func=ACT.Square)

        def jn(s, k):
            nc.vector.tensor_tensor(out=packed(m_bf[:, s % 3, k]), in0=pairs(z[s, 1 + k][:]), in1=pairs(sg[s][:]), op=ALU.mult)

        def q_add(s, k, name):
            eng = ALUS[name]
            if k == 1:
                q[s] = work.tile([P, 512], F32, name="q%d" % s, tag="q", bufs=1)
                eng.tensor_tensor(out=q[s][:], in0=sq[s, 0][:], in1=sq[s, 1][:], op=ALU.add)
            else:
                eng.tensor_tensor(out=q[s][:], in0=q[s][:], in1=sq[s, 2][:], op=ALU.add)

        def aq(s, name):
            m[s] = work.tile([P, 512], F32, name="m%d" % s, tag="m")
            ALUS[name].tensor_tensor(out=m[s][:], in0=q[s][:], in1=a[s][:], op=ALU.mult)

        def lap_sum(s):
            r[s] = work.tile([P, 512], F32, name="r%d" % s, tag="r")
            nc.vector.scalar_tensor_tensor(
                out=r[s][:], in0=m[s][:], scalar=-2.0, in1=z[s, 4][:], op0=ALU.mult, op1=ALU.add)

        def ln(s):
            nc.vector.tensor_tensor(out=packed(m_bf[:, (s + 1) % 3, 3]), in0=pairs(r[s][:]), in1=pairs(sg[s][:]), op=ALU.mult)

        def rows(ap, hf):
            return ap.rearrange("p (f b) -> p f b", f=4)[:, :, 64 * hf : 64 * hf + 64]

        def aq_half(s, hf):
            m[s, hf] = work.tile([P, 4, 64], F32, name="mh%d" % hf, tag="mh")
            nc.vector.tensor_tensor(out=m[s, hf][:], in0=rows(q[s][:], hf), in1=rows(a[s][:], hf), op=ALU.mult)

        def lap_half(s, hf):
            r[s, hf] = work.tile([P, 4, 64], F32, name="rh%d" % hf, tag="rh")
            nc.vector.scalar_tensor_tensor(
                out=r[s, hf][:], in0=m[s, hf][:], scalar=-2.0, in1=rows(z[s, 4][:], hf), op0=ALU.mult, op1=ALU.add)

        def ln_half(s, hf):
            cs = slice(32 * hf, 32 * hf + 32)
            nc.vector.tensor_tensor(out=packed(m_bf[:, (s + 1) % 3, 3])[:, cs], in0=r[s, hf][:].rearrange("p f (c i) -> p c f i", i=2), in1=pairs(sg[s][:])[:, cs], op=ALU.mult)

        def m_quant(s, k0, k1):
            nc.vector.quantize_mx(
                out=m_codes[:, s, k0:k1].rearrange("p k c -> p (k c)").bitcast(X4),
                scales=m_scales[:, s, k0:k1].rearrange("p k c -> p (k c)"),
                in_=m_bf[:, s % 3, k0:k1].rearrange("p k c -> p (k c)"),
            )

        o, e, u = {}, {}, {}

        def o_mm(t, k, bk, turned):
            ps = bank(bk, "o%d_%d" % (t, k))
            o[t, k] = ps
            if not turned:
                for G in range(2):
                    nc.tensor.matmul_mx(
                        out=ps[:], lhsT=m_codes[:, 2 * t + G + k // 3, k].bitcast(X4), lhsT_scale=m_scales[:, 2 * t + G + k // 3, k],
                        rhs=w_codes[:, 4 + G].bitcast(X4), rhs_scale=w_scales[:, 4 + G],
                        start=(G == 0), stop=(G == 1))
                return
            for c in range(4):
                cols = slice(c * P, (c + 1) * P)
                for G in range(2):
                    nc.tensor.matmul_mx(
                        out=ps[:, cols], lhsT=w_codes[:, 4 + G, cols].bitcast(X4), lhsT_scale=w_scales[:, 4 + G, cols],
                        rhs=m_codes[:, 2 * t + G + k // 3, k].bitcast(X4), rhs_scale=m_scales[:, 2 * t + G + k // 3, k],
                        start=(G == 0), stop=(G == 1))

        def o_sq(t, k):
            e[t, k] = work.tile([P, PO], F32, name="e%d_%d" % (t, k), tag="e%d" % k, bufs=1)
            nc.scalar.activation(out=e[t, k][:], in_=o[t, k][:], func=ACT.Square, scale=math.sqrt(0.5))

        def turn_sum(ps, terms):
            for c in range(4):
                cols = slice(c * P, (c + 1) * P)
                for n, term in enumerate(terms):
                    nc.tensor.matmul(out=ps[:, cols], lhsT=term[:, cols], rhs=ident[:], start=(n == 0), stop=(n == len(terms) - 1), is_transpose=True)

        ea, qa, qt = {}, {}, {}

        def e_turn(t, bk):
            ea[t] = bank(bk, "ea%d" % t)
            turn_sum(ea[t], [e[t, k] for k in range(3)])

        def e_copy(t):
            u[t] = work.tile([P, PO], F32, name="u%d" % t, tag="u", bufs=1)
            nc.scalar.copy(out=u[t][:], in_=ea[t][:])

        def q_turn(s, bk):
            qa[s] = bank(bk, "qa%d" % s)
            turn_sum(qa[s], [sq[s, k] for k in range(3)])

        def q_copy(s):
            qt[s] = work.tile([P, 512], F32, name="qt%d" % s, tag="qt", bufs=1)
            nc.scalar.copy(out=qt[s][:], in_=qa[s][:])

        def q_back(s, bk):
            q[s] = bank(bk, "qb%d" % s)
            turn_sum(q[s], [qt[s]])

        def e_add(t, k, name):
            if k == 1:
                u[t] = work.tile([P, PO], F32, name="u%d" % t, tag="u", bufs=1)
                ALUS[name].tensor_tensor(out=u[t][:], in0=e[t, 0][:], in1=e[t, 1][:], op=ALU.add)
            else:
                ALUS[name].tensor_tensor(out=u[t][:], in0=u[t][:], in1=e[t, 2][:], op=ALU.add)

        def finish(t, c0=0, c1=PO):
            nc.vector.scalar_tensor_tensor(
                out=res[:, t, c0:c1], in0=o[t, 3][:, c0:c1], scalar=-0.5, in1=u[t][:, c0:c1], op0=ALU.mult, op1=ALU.subtract)

        oh = {}

        def o_half(hf, bk):
            oh[hf] = bank(bk, "oh%d" % hf)
            cols = slice(256 * hf, 256 * hf + 256)
            for G in range(2):
                nc.tensor.matmul_mx(
                    out=oh[hf][:, 0:256], lhsT=m_codes[:, 7 + G, 3].bitcast(X4), lhsT_scale=m_scales[:, 7 + G, 3],
                    rhs=w_codes[:, 4 + G, cols].bitcast(X4), rhs_scale=w_scales[:, 4 + G, cols],
                    start=(G == 0), stop=(G == 1))

        def finish_half(hf):
            cols = slice(256 * hf, 256 * hf + 256)
            nc.vector.scalar_tensor_tensor(
                out=res[:, 3, cols], in0=oh[hf][:, 0:256], scalar=-0.5, in1=u[3][:, cols], op0=ALU.mult, op1=ALU.subtract)

        def store(t0, t1):
            nc.sync.dma_start(out=out_0.rearrange("(p t) m -> p t m", t=4)[:, t0:t1, :], in_=res[:, t0:t1, :])

        def res_cast(c0, c1, eng):
            copy_on(eng, res_bf[:, 4 * c0 : 4 * c1].rearrange("p (c i t) -> p c t i", t=4, i=2), res[:, :, c0:c1].rearrange("p t (c i) -> p c t i", i=2))

        def res_quant(c0, c1):
            nc.vector.quantize_mx(out=res_codes[:, c0:c1].bitcast(X4), scales=res_scales[:, c0:c1], in_=res_bf[:, 4 * c0 : 4 * c1])

        make_identity(nc, ident[:])
        nc.gpsimd.dma_start(out=b_bf[:], in_=b1.rearrange("(G p f) -> p G f", G=2, f=4))
        nc.gpsimd.dma_start(out=g_bf[:], in_=g.rearrange("(G p f) -> p G f", G=2, f=4))
        nc.gpsimd.tensor_scalar(out=g_neg[:], in0=g_bf[:], scalar1=-1.0, scalar2=0.0, op0=ALU.mult, op1=ALU.add)
        nc.gpsimd.tensor_scalar(out=g_pos[:], in0=g_bf[:], scalar1=1.0, scalar2=0.0, op0=ALU.mult, op1=ALU.add)
        load_j(0, 1, 2)
        load_h(0)
        load_w1(0, 1)
        load_w1(0, 0)
        load_j(0, 0, 1)
        load_l(0)
        load_h(1)
        load_j(0, 2, 3)
        load_w1(1, 0)
        load_w1(1, 1)
        load_j(1, 1, 2)
        load_j(1, 2, 3)
        load_j(1, 0, 1)
        load_l(2)
        load_l(1)
        load_j(2, 1, 2)
        load_w2(0)
        load_j(3, 1, 2)
        load_h(2)
        load_j(3, 2, 3)
        load_j(2, 2, 3)
        load_h(3)
        load_w2(1)
        load_j(3, 0, 1)
        load_j(2, 0, 1)
        load_l(3)
        nc.vector.memset(zeros[:], 0.0)
        nc.vector.memset(warm[:], 0.0)
        keep_warm(4)
        nc.scalar.activation(out=warm[:], in_=warm[:], func=ACT.Tanh)
        x_turn(0, 2, 0)
        keep_warm(1)
        x_turn(0, 0, 1)
        keep_warm(7)
        x_turn(0, 1, 2)
        x_turn(0, 4, 3)
        keep_warm(1)
        x_copy(0, 2, "v")
        w_inter(1, "s", 1)
        w_inter(1, "v", 0)
        w_inter(0, "s", 0)
        x_turn(1, 0, 4)
        x_copy(0, 1, "s")
        x_copy(0, 0, "v")
        w_inter(0, "v", 1)
        w_quant(1)
        x_quant(0, 0, 1)
        x_copy(0, 4, "s")
        w_quant(0)
        x_quant(0, 1, 3)
        x_copy(1, 0, "s")
        x_turn(0, 3, 5)
        x_copy(0, 3, "s")
        z_mm(0, 0, 6)
        w_inter(2, "v", 0)
        x_quant(1, 0, 1)
        tanh(0)
        x_quant(0, 3, 5)
        z_mm(0, 1, 7)
        z_mm(0, 2, 0)
        w_inter(2, "v", 1)
        z_sq(0, 0)
        z_mm(2, 0, 2)
        z_mm(0, 3, 1)
        x_turn(1, 3, 3)
        a_sq(0, "s")
        z_sq(0, 1)
        w_inter(3, "s", 0)
        z_sq(0, 2)
        x_turn(1, 1, 4)
        tanh(2)
        w_inter(3, "v", 1)
        x_copy(1, 3, "s")
        w_quant(2)
        q_add(0, 1, "v")
        x_turn(1, 4, 5)
        x_turn(1, 2, 6)
        slope(0, "v")
        w_quant(3)
        z_mm(1, 1, 2)
        z_mm(1, 0, 3)
        x_copy(1, 1, "s")
        q_add(0, 2, "v")
        x_copy(1, 2, "s")
        x_copy(1, 4, "s")
        w_inter(4, "v", 0)
        jn(0, 2)
        jn(0, 0)
        aq(0, "g")
        x_turn(2, 0, 4)
        tanh(1)
        jn(0, 1)
        z_mm(0, 4, 6)
        z_mm(3, 0, 5)
        m_quant(0, 2, 3)
        w_inter(4, "v", 1)
        x_quant(1, 1, 5)
        lap_sum(0)
        a_sq(2, "s")
        z_mm(1, 3, 1)
        x_copy(2, 0, "v")
        z_mm(1, 2, 7)
        x_turn(2, 4, 3)
        a_sq(1, "s")
        w_quant(4)
        x_turn(2, 2, 0)
        tanh(3)
        z_mm(2, 2, 6)
        z_mm(2, 1, 4)
        z_sq(1, 0)
        z_sq(1, 1)
        q_add(1, 1, "v")
        x_copy(2, 4, "s")
        z_sq(1, 2)
        z_mm(2, 3, 5)
        slope(1, "g")
        z_mm(1, 4, 3)
        m_quant(0, 0, 2)
        jn(1, 2)
        slope(2, "s")
        x_copy(2, 2, "s")
        x_turn(3, 4, 1)
        x_turn(2, 1, 0)
        jn(1, 0)
        jn(1, 1)
        a_sq(3, "s")
        x_quant(2, 0, 1)
        q_add(1, 2, "g")
        z_sq(2, 0)
        z_sq(2, 1)
        w_inter(5, "v", 0)
        x_copy(3, 4, "s")
        aq(1, "v")
        ln(0)
        jn(2, 1)
        q_add(2, 1, "g")
        z_sq(2, 2)
        x_turn(3, 3, 2)
        jn(2, 0)
        lap_sum(1)
        x_turn(2, 3, 7)
        m_quant(1, 0, 4)
        z_mm(3, 2, 1)
        z_mm(4, 0, 6)
        w_inter(5, "s", 1)
        x_copy(2, 3, "s")
        ln(1)
        x_turn(3, 1, 4)
        w_quant(5)
        tanh(4)
        x_turn(3, 0, 3)
        x_turn(3, 2, 7)
        q_add(2, 2, "v")
        x_copy(2, 1, "s")
        z_mm(3, 1, 6)
        slope(3, "s")
        z_mm(3, 3, 0)
        x_copy(3, 3, "s")
        aq(2, "g")
        o_mm(0, 2, 2, True)
        x_quant(2, 1, 5)
        x_copy(3, 0, "s")
        z_mm(2, 4, 3)
        x_copy(3, 1, "s")
        z_sq(3, 1)
        o_mm(0, 1, 4, True)
        jn(3, 2)
        jn(2, 2)
        jn(3, 1)
        lap_sum(2)
        z_sq(3, 0)
        z_mm(5, 3, 5)
        x_copy(3, 2, "s")
        o_sq(0, 2)
        z_sq(3, 2)
        z_mm(4, 2, 1)
        jn(3, 0)
        o_mm(0, 0, 3, True)
        q_add(3, 1, "g")
        a_sq(4, "s")
        o_sq(0, 1)
        z_mm(4, 1, 7)
        slope(4, "s")
        ln(2)
        z_mm(5, 2, 2)
        o_sq(0, 0)
        q_add(3, 2, "v")
        z_sq(4, 1)
        z_mm(5, 0, 0)
        z_mm(3, 4, 6)
        x_quant(3, 1, 5)
        tanh(5)
        aq(3, "v")
        m_quant(3, 0, 4)
        z_mm(4, 3, 4)
        e_turn(0, 3)
        m_quant(2, 0, 4)
        x_quant(3, 0, 1)
        jn(4, 1)
        z_sq(4, 0)
        jn(4, 0)
        a_sq(5, "s")
        lap_sum(3)
        z_sq(4, 2)
        z_mm(5, 1, 0)
        q_add(4, 1, "g")
        o_mm(1, 0, 1, True)
        slope(5, "s")
        z_mm(6, 2, 7)
        e_copy(0)
        z_mm(4, 4, 6)
        q_add(4, 2, "v")
        o_sq(1, 0)
        ln(3)
        z_mm(6, 0, 3)
        aq(4, "g")
        z_sq(5, 0)
        jn(4, 2)
        jn(5, 0)
        z_sq(5, 1)
        o_mm(1, 1, 1, True)
        jn(5, 1)
        z_sq(6, 1)
        z_sq(5, 2)
        lap_sum(4)
        o_mm(1, 2, 4, True)
        tanh(6)
        z_mm(7, 0, 0)
        o_sq(1, 1)
        z_mm(7, 3, 2)
        a_sq(6, "s")
        z_mm(6, 3, 6)
        q_add(5, 1, "g")
        z_mm(5, 4, 3)
        o_mm(0, 3, 1, False)
        jn(5, 2)
        ln(4)
        tanh(7)
        m_quant(4, 0, 4)
        q_add(5, 2, "v")
        aq(5, "g")
        m_quant(5, 0, 4)
        finish(0)
        store(0, 1)
        z_mm(6, 1, 5)
        slope(6, "s")
        o_sq(1, 2)
        jn(6, 2)
        a_sq(7, "s")
        z_mm(7, 2, 0)
        z_mm(7, 1, 1)
        jn(6, 1)
        z_sq(6, 0)
        lap_sum(5)
        e_turn(1, 4)
        jn(6, 0)
        slope(7, "s")
        o_mm(2, 1, 7, True)
        z_sq(6, 2)
        q_add(6, 1, "g")
        jn(7, 2)
        z_sq(7, 0)
        jn(7, 1)
        q_add(6, 2, "g")
        jn(7, 0)
        o_mm(2, 0, 3, True)
        z_mm(6, 4, 5)
        o_mm(2, 2, 6, True)
        ln(5)
        o_sq(2, 1)
        o_sq(2, 0)
        z_sq(7, 1)
        o_mm(1, 3, 1, False)
        m_quant(7, 2, 3)
        aq(6, "v")
        o_sq(2, 2)
        e_copy(1)
        z_sq(7, 2)
        z_mm(7, 4, 7)
        m_quant(6, 0, 4)
        lap_sum(6)
        q_add(7, 1, "g")
        finish(1)
        store(1, 2)
        e_turn(2, 3)
        m_quant(7, 1, 2)
        m_quant(7, 0, 1)
        q_add(7, 2, "v")
        o_mm(3, 2, 0, True)
        o_mm(3, 1, 6, True)
        o_mm(3, 0, 4, True)
        ln(6)
        aq_half(7, 1)
        aq_half(7, 0)
        lap_half(7, 1)
        o_mm(2, 3, 2, False)
        e_copy(2)
        lap_half(7, 0)
        o_sq(3, 2)
        ln_half(7, 1)
        o_sq(3, 1)
        ln_half(7, 0)
        finish(2)
        o_sq(3, 0)
        e_turn(3, 5)
        m_quant(8, 3, 4)
        m_quant(7, 3, 4)
        e_copy(3)
        o_half(1, 1)
        finish_half(1)
        o_half(0, 3)
        finish_half(0)
        store(2, 4)
        res_cast(256, 384, "v")
        res_cast(384, 512, "s")
        res_cast(128, 256, "v")
        res_cast(0, 128, "v")
        res_quant(256, 512)
        res_quant(0, 256)
        nc.sync.dma_start(out=out_1[0].rearrange("p m t -> p (m t)").bitcast(I32), in_=res_codes[:].bitcast(I32))
        for Q in range(4):
            eng = nc.scalar if Q % 2 else nc.sync
            eng.dma_start(out=out_2[0, 4 * Q : 4 * Q + 4, :].bitcast(I32), in_=res_scales[32 * Q : 32 * Q + 4, :].bitcast(I32))
